import numpy as np
import ml_dtypes


def mxq(x, axis, fmt="e4m3"):
    dtype, down = {"e4m3": (ml_dtypes.float8_e4m3fn, 7), "e5m2": (ml_dtypes.float8_e5m2, 14)}[fmt]
    v = np.moveaxis(np.asarray(x, np.float32).astype(ml_dtypes.bfloat16).astype(np.float64), axis, -1)
    blocks = v.reshape(v.shape[:-1] + (-1, 32))
    amax = np.abs(blocks).max(-1, keepdims=True)
    byte = np.maximum(np.where(amax > 0, np.frexp(amax)[1] - 1 + 127, 0) - down, 1)
    scale = np.exp2(byte - 127.0)
    codes = (blocks / scale).astype(np.float32).astype(dtype).astype(np.float64)
    return np.moveaxis((codes * scale).reshape(v.shape), -1, axis)


WIDE = False


def mx_kscale(k):
    if not WIDE:
        return np.ones(k)
    levels = np.array([10, -10, 5, -5, 0])
    if k % 512:
        return np.exp2(np.random.permutation(np.resize(levels, k // 32))).repeat(32)
    a = np.empty((k // 512, 16))
    for p in range(k // 512):
        a[p, :8] = np.random.permutation(np.resize(levels, 8))
        for g in range(8):
            far = levels[np.abs(levels - a[p, g]) >= 10]
            a[p, g + 8] = far[np.random.randint(len(far))]
    return np.exp2(a.ravel()).repeat(32)


BF16 = ml_dtypes.bfloat16


def bf(x):
    return np.asarray(x, np.float32).astype(BF16)


def f64(x):
    return np.asarray(x).astype(np.float64)


E2M1 = np.array([0.0, 0.5, 1.0, 1.5, 2.0, 3.0, 4.0, 6.0, -0.0, -0.5, -1.0, -1.5, -2.0, -3.0, -4.0, -6.0])


def pack_weight(w, fmt):
    k, n = w.shape
    w = f64(bf(w)).reshape(k // 32, 32, n)
    amax = np.abs(w).max(1)
    if fmt == "e4m3":
        byte = np.frexp(amax)[1] - 1 + 127 - 7
    else:
        mant, ex = np.frexp(amax / 6.0)
        byte = np.where(mant > 0.5, ex, ex - 1) + 127
    byte = np.clip(np.where(amax > 0, byte, 1), 1, 254)
    scaled = (w * np.exp2(127.0 - byte)[:, None, :]).reshape(k, n).astype(np.float32)
    by_word = np.ascontiguousarray(scaled.reshape(k // 512, 128, 4, n).transpose(0, 1, 3, 2))
    if fmt == "e4m3":
        words = by_word.astype(ml_dtypes.float8_e4m3fn).view(np.uint8)
    else:
        c = by_word.astype(ml_dtypes.float4_e2m1fn).view(np.uint8) & 0xF
        words = c[..., 0::2] | (c[..., 1::2] << 4)
    return np.ascontiguousarray(words), np.ascontiguousarray(byte.astype(np.uint8).reshape(k // 512, 16, n))


def unpack_weight(words, scales, fmt):
    g, p, n, _ = words.shape
    if fmt == "e4m3":
        vals = np.ascontiguousarray(words).view(ml_dtypes.float8_e4m3fn).astype(np.float64)
    else:
        nib = np.empty((g, p, n, 4), np.uint8)
        nib[..., 0::2] = words & 0xF
        nib[..., 1::2] = words >> 4
        vals = E2M1[nib]
    vals = vals * np.repeat(np.exp2(scales.astype(np.float64) - 127.0), 8, axis=1)[..., None]
    return vals.transpose(0, 1, 3, 2).reshape(g * 512, n)
def pack4(w):
    words, scales = pack_weight(w, "e2m1")
    return words.reshape(words.shape[0], 128, -1), scales


def unpack4(words, scales):
    return unpack_weight(words.reshape(words.shape[0], 128, -1, 2), scales, "e2m1")


N, D, H, E = 512, 1024, 4, 512
HE = H * E


def draw0():
    s, t = mx_kscale(D), mx_kscale(HE)
    x = bf((np.random.standard_normal((N, D)) + 0.5 * np.random.standard_normal((1, D))) * s[None, :])
    w_q_words, w_q_scales = pack4(np.random.standard_normal((D, HE)) / np.sqrt(D) / s[:, None])
    g_q = bf((1.0 + 0.1 * np.random.standard_normal(HE)) * t)
    w_k_words, w_k_scales = pack4(np.random.standard_normal((D, HE)) / np.sqrt(D) / s[:, None] / t[None, :])
    return {
        "x": x,
        "w_q_words": w_q_words,
        "w_q_scales": w_q_scales,
        "g_q": g_q,
        "w_k_words": w_k_words,
        "w_k_scales": w_k_scales,
        "w_head": bf(np.random.uniform(0.3, 0.8, H)),
        "b_head": bf(0.5 + 0.1 * np.random.standard_normal(1)),
    }


def attention_maps(q, k):
    qq = mxq(q.transpose(1, 0, 2), 2, "e4m3")
    kq = mxq(k.transpose(1, 2, 0), 1, "e4m3")
    logits = (qq @ kq) / np.sqrt(E)
    e = np.exp(logits - logits.max(axis=-1, keepdims=True))
    return e / e.sum(axis=-1, keepdims=True)


def average_product_correction(s):
    r = np.sum(s, axis=-1)
    t = np.sum(r, axis=-1)
    background = r[:, :, None] * r[:, None, :] / t[:, None, None]
    return s - background


def core(x, w_q_words, w_q_scales, g_q, w_k_words, w_k_scales, w_head, b_head):
    n = x.shape[0]
    heads = w_head.shape[0]
    xq = mxq(f64(x), 1, "e4m3")
    q = ((xq @ unpack4(w_q_words, w_q_scales)) * f64(g_q)[None, :]).reshape(n, heads, E)
    k = (xq @ unpack4(w_k_words, w_k_scales)).reshape(n, heads, E)
    a = attention_maps(q, k)
    s = a + np.swapaxes(a, -1, -2)
    c = average_product_correction(s)
    weights = n * f64(w_head)
    logit = f64(b_head)[0] + np.sum(weights[:, None, None] * c, axis=0)
    return 1.0 / (1.0 + np.exp(-logit))


def e4m3fn_bytes(y):
    return np.clip(np.asarray(y, np.float64), -448.0, 448.0).astype(np.float32).astype(ml_dtypes.float8_e4m3fn).view(np.uint8)


def e4m3fn_values(b):
    return np.asarray(b, np.uint8).view(ml_dtypes.float8_e4m3fn).astype(np.float64)


def setup_inputs():
    d = draw0()
    x0 = np.asarray(d['x']).astype(np.float64)
    s = (np.max(np.abs(x0), axis=(0,), keepdims=True) / 448.0).astype(np.float32)
    out = {}
    for k, v in d.items():
        if k == 'x':
            out['x_bytes'] = e4m3fn_bytes(x0 / s.astype(np.float64))
            out['x_scale'] = s
        else:
            out[k] = v
    return out


def reference(x_bytes, x_scale, w_q_words, w_q_scales, g_q, w_k_words, w_k_scales, w_head, b_head):
    return core(e4m3fn_values(x_bytes) * x_scale.astype(np.float64), w_q_words, w_q_scales, g_q, w_k_words, w_k_scales, w_head, b_head)

@@ -1,0 +1,655 @@
+from contextlib import ExitStack
+
+import concourse.mybir as mybir
+from concourse.masks import make_identity
+
+N, D, H, E = 512, 1024, 4, 512
+FLOPS = 2 * (2 * N * D * H * E) + H * 2 * N * N * E
+
+F32 = mybir.dt.float32
+BF16 = mybir.dt.bfloat16
+I32 = mybir.dt.int32
+U32 = mybir.dt.uint32
+U8 = mybir.dt.uint8
+FP8 = mybir.dt.float8_e4m3fn
+FP8X4 = mybir.dt.float8_e4m3fn_x4
+FP4X4 = mybir.dt.float4_e2m1fn_x4
+ALU = mybir.AluOpType
+ACT = mybir.ActivationFunctionType
+AX = mybir.AxisListType
+
+P = 128
+T = 4
+G = D // 512
+R = N // P
+S = H * R
+SCALE = 1.0 / E**0.5
+
+
+def tile_esmcontactheadapc_w4_kernel(
+    tc, x_bytes, x_scale, w_q_words, w_q_scales, g_q, w_k_words, w_k_scales, w_head, b_head, out
+):
+    nc = tc.nc
+    with ExitStack() as ctx:
+        keep = ctx.enter_context(tc.tile_pool(name="keep", bufs=1))
+        psum = ctx.enter_context(tc.psum_pool(name="psum", bufs=1))
+        ctx.enter_context(tc.manual_schedule())
+
+        def sb(name, shape, dtype, align=64):
+            return keep.tile(shape, dtype, name=name, align_bytes=align)
+
+        BUFS = {"p": 3, "l": 3, "t": 2}
+
+        def bank(name, tag, shape=(P, 512), dtype=F32):
+            return psum.tile(list(shape), dtype, name=name, tag=tag, bufs=BUFS[tag])
+
+        xb = [sb(f"xb{i}", [P, D], U8) for i in range(R)]
+        xscale = sb("xscale", [P, D], F32)
+        xs = [sb(f"xs{i}", [P, D], BF16) for i in range(R)]
+        xg = [sb(f"xg{i}", [P, G, P, T], BF16) for i in range(R)]
+        xc = sb("xc", [P, G, N], U32)
+        xcs = sb("xcs", [P, G, N], U8)
+        words = {"q": w_q_words, "k": w_k_words}
+        scales = {"q": w_q_scales, "k": w_k_scales}
+        wraw = {(s, j): sb(f"wraw_{s}{j}", [P, G, 2048], U8) for s in "qk" for j in range(2)}
+        wp = {(s, j): sb(f"wp_{s}{j}", [P, T, G, 512], U8) for s in "qk" for j in range(2)}
+        sraw = {s: sb(f"sraw_{s}", [P, G, H * E], U8) for s in "qk"}
+        sp = {s: sb(f"sp_{s}", [P, T, G, H * P], U8) for s in "qk"}
+        grp = {(s, h): sb(f"grp_{s}{h}", [P, N, T], BF16) for s in "qk" for h in range(H)}
+        code = {(s, h): sb(f"code_{s}{h}", [P, N], U32) for s in "qk" for h in range(H)}
+        cscl = {(s, h): sb(f"cscl_{s}{h}", [P, N], U8) for s in "qk" for h in range(H)}
+        flat = {h: sb(f"flat{h}", [P, T, N], BF16) for h in []}
+        e = {(h, i): sb(f"e{h}{i}", [P, N], F32) for h in range(H) for i in range(R)}
+        p = {(h, i): sb(f"p{h}{i}", [P, N], F32) for h in range(H) for i in range(R)}
+        acc = [sb(f"acc{i}", [P, N], F32) for i in range(R)]
+        junk = [sb(f"junk{i}", [P, N], BF16) for i in range(2)]
+        ident = sb("ident", [P, P], F32)
+        ident16 = sb("ident16", [P, P], BF16)
+        g_rows = sb("g_rows", [P, P], BF16)
+        gain = sb("gain", [P, H, T], F32)
+        w_bf = sb("w_bf", [P, H], BF16)
+        b_bf = sb("b_bf", [P, 1], BF16)
+        w_pos = sb("w_pos", [P, H], F32)
+        w_inv = sb("w_inv", [P, H], F32)
+        bias = sb("bias", [P, 1], F32)
+        zero = sb("zero", [P, 1], F32)
+        dummy = sb("dummy", [P, 1], F32)
+        rowmax = sb("rowmax", [P, S], F32)
+        nbias = sb("nbias", [P, S], F32)
+        rowsum = sb("rowsum", [P, S], F32)
+        rinv = sb("rinv", [P, S], F32)
+        pcol = sb("pcol", [P, S], F32)
+        plast = sb("plast", [P, R, R], F32)
+        uvt = [sb(f"uvt{k}", [P, R, P], BF16) for k in range(2)]
+        ru = sb("ru", [P, N], BF16)
+        rv = sb("rv", [P, N], BF16)
+        res = [sb(f"res{i}", [P, N], F32) for i in range(R)]
+        osb = [sb(f"osb{i}", [P, N], F32) for i in range(R)]
+
+        def load_x(i):
+            nc.sync.dma_start(out=xb[i][:], in_=x_bytes[i * P : (i + 1) * P, :])
+
+        def load_w(s, j):
+            nc.sync.dma_start(
+                out=wraw[s, j][:], in_=words[s][:, :, j * 2048 : (j + 1) * 2048].rearrange("g p c -> p g c")
+            )
+
+        def load_s(s):
+            for q in range(4):
+                nc.sync.dma_start(
+                    out=sraw[s][32 * q : 32 * q + 4].bitcast(I32),
+                    in_=scales[s].bitcast(I32)[:, 4 * q : 4 * q + 4, :].rearrange("g q n -> q g n"),
+                )
+
+        nc.vector.memset(sraw["k"][:].rearrange("p g c -> p (g c)").bitcast(I32), 0)
+        nc.vector.memset(zero[:], 0.0)
+        nc.vector.memset(sraw["q"][:].rearrange("p g c -> p (g c)").bitcast(I32), 0)
+        make_identity(nc, ident[:])
+        nc.gpsimd.memset(g_rows[:], 0.0)
+        nc.gpsimd.memset(uvt[0][:], 0.0)
+        nc.gpsimd.memset(uvt[1][:], 0.0)
+
+        nc.scalar.dma_start(out=xscale[:], in_=x_scale.rearrange("o k -> (o k)").partition_broadcast(P))
+        nc.scalar.activation(out=dummy[:], in_=zero[:], func=ACT.Exp)
+        load_x(0)
+        load_x(1)
+        load_w("k", 0)
+        load_s("k")
+        load_x(2)
+        load_x(3)
+        load_s("q")
+        load_w("q", 0)
+        load_w("k", 1)
+        load_w("q", 1)
+        for h in range(H):
+            nc.scalar.dma_start(
+                out=g_rows[T * h : T * (h + 1), :].rearrange("t (b i) -> t b i", i=8),
+                in_=g_q[E * h : E * (h + 1)].rearrange("(b t i) -> t b i", t=T, i=8),
+            )
+        nc.scalar.dma_start(out=w_bf[:], in_=w_head.partition_broadcast(P))
+        nc.scalar.dma_start(out=b_bf[:], in_=b_head.partition_broadcast(P))
+        nc.vector.tensor_copy(out=ident16[:], in_=ident[:])
+
+        def mult_x(i):
+            nc.vector.tensor_tensor(out=xs[i][:], in0=xb[i][:].bitcast(FP8), in1=xscale[:], op=ALU.mult)
+
+        xts = {}
+
+        def turn_x(i):
+            w = xs[i][:].bitcast(F32)
+            xts[i] = bank(f"xt{i}", "l", (P, G, 2, P))
+            for g in range(G):
+                for u in range(2):
+                    nc.tensor.transpose(xts[i][:, g, u, :], w[:, 256 * g + u : 256 * (g + 1) : 2], ident[:])
+
+        def pack_x(i):
+            nc.scalar.copy(out=xg[i][:].bitcast(F32), in_=xts[i][:].rearrange("p g u r -> p g r u"))
+
+        def quant_x(i):
+            for g in range(G):
+                r = slice(i * P, (i + 1) * P)
+                nc.vector.quantize_mx(
+                    out=xc[:, g, r].bitcast(FP8X4), scales=xcs[:, g, r], in_=xg[i][:, g].rearrange("p r t -> p (r t)")
+                )
+
+        def perm_w(s, j):
+            nc.vector.tensor_copy(
+                out=wp[s, j][:].rearrange("p t g c -> p t (g c)").bitcast(I32).rearrange("p t (b i) -> p t b i", i=4),
+                in_=wraw[s, j][:].rearrange("p g c -> p (g c)").bitcast(I32).rearrange("p (b t i) -> p t b i", t=T, i=4),
+            )
+
+        def perm_s(s):
+            nc.vector.tensor_copy(
+                out=sp[s][:].rearrange("p t g c -> p t (g c)").bitcast(I32).rearrange("p t (b i) -> p t b i", i=2),
+                in_=sraw[s][:].rearrange("p g c -> p (g c)").bitcast(I32).rearrange("p (b t i) -> p t b i", t=T, i=2),
+            )
+
+        def mx(dst, s, h, t, lo, hi):
+            c = 256 * (h % 2)
+            for g in range(G):
+                nc.tensor.matmul_mx(
+                    out=dst,
+                    lhsT=wp[s, h // 2][:, t, g, c : c + 256].bitcast(FP4X4),
+                    lhsT_scale=sp[s][:, t, g, h * P : (h + 1) * P],
+                    rhs=xc[:, g, lo:hi].bitcast(FP8X4),
+                    rhs_scale=xcs[:, g, lo:hi],
+                    start=(g == 0),
+                    stop=(g == G - 1),
+                )
+
+        pss = {}
+
+        def proj(s, h, i):
+            if s == "q" and h in flat:
+                pss[s, h, i] = bank(f"pq_{h}{i}", "p")
+                mx(pss[s, h, i][:], s, h, i, 0, N)
+                return
+            pss[s, h, i] = bank(f"ps_{s}{h}{i}", "p", (P, T, P))
+            for t in range(T):
+                mx(pss[s, h, i][:, t, :], s, h, t, i * P, (i + 1) * P)
+
+        def empty(s, h, i):
+            ps = pss[s, h, i]
+            if s == "q" and h in flat:
+                nc.scalar.activation(out=flat[h][:, i, :], in_=ps[:], func=ACT.Copy, scale=gain[:, h, i : i + 1])
+                return
+            dst = grp[s, h][:, i * P : (i + 1) * P, :]
+            src = ps[:].rearrange("p t n -> p n t")
+            if s == "k":
+                nc.scalar.copy(out=dst, in_=src)
+            else:
+                nc.vector.tensor_tensor(
+                    out=dst, in0=src, in1=gain[:, h : h + 1, :].to_broadcast([P, P, T]), op=ALU.mult
+                )
+
+        def weave(h, lo, hi):
+            if h in flat:
+                src = flat[h][:, :, lo:hi].rearrange("p t n -> p n t")
+                nc.vector.tensor_copy(out=grp["q", h][:, lo:hi, :], in_=src)
+
+        def quant(s, h, lo, hi):
+            nc.vector.quantize_mx(
+                out=code[s, h][:, lo:hi].bitcast(FP8X4),
+                scales=cscl[s, h][:, lo:hi],
+                in_=grp[s, h][:, lo:hi, :].rearrange("p n t -> p (n t)"),
+            )
+
+        logits = {}
+
+        def score(h, i):
+            lg = bank(f"lg{h}{i}", "l")
+            r = slice(i * P, (i + 1) * P)
+            nc.tensor.matmul_mx(
+                out=lg[:],
+                lhsT=code["q", h][:, r].bitcast(FP8X4),
+                lhsT_scale=cscl["q", h][:, r],
+                rhs=code["k", h][:].bitcast(FP8X4),
+                rhs_scale=cscl["k", h][:],
+                start=True,
+                stop=True,
+            )
+            logits[h, i] = lg
+
+        def row_max(h, i):
+            c = h * R + i
+            nc.vector.tensor_reduce(out=rowmax[:, c : c + 1], in_=logits[h, i][:], axis=AX.X, op=ALU.max)
+
+        def negate(h, i):
+            c = h * R + i
+            nc.scalar.activation(out=nbias[:, c : c + 1], in_=rowmax[:, c : c + 1], func=ACT.Copy, scale=-SCALE)
+
+        def expo(h, i):
+            c = h * R + i
+            nc.scalar.activation(
+                out=e[h, i][:], in_=logits[h, i][:], func=ACT.Exp, bias=nbias[:, c : c + 1], scale=SCALE,
+                accum_out=rowsum[:, c : c + 1],
+            )
+
+        def recip(h, i):
+            c = h * R + i
+            nc.vector.reciprocal(rinv[:, c : c + 1], rowsum[:, c : c + 1])
+
+        def weigh(h, i):
+            c = h * R + i
+            eng = nc.gpsimd if h < H - 1 else nc.vector
+            eng.tensor_scalar(
+                out=p[h, i][:], in0=e[h, i][:], scalar1=rinv[:, c : c + 1], scalar2=w_pos[:, h : h + 1],
+                op0=ALU.mult, op1=ALU.mult,
+            )
+
+        def gather(h, i):
+            eng = nc.vector if (h, i) in [(3, 3),(3, 2)] else nc.gpsimd
+            first = p[0, i] if h == 1 else acc[i]
+            eng.tensor_tensor(out=acc[i][:], in0=first[:], in1=p[h, i][:], op=ALU.add)
+
+        tps = {}
+
+        def turn_p(h, j):
+            tps[h, j] = bank(f"tp{h}{j}", "p" if h == H - 2 else "t")
+            for i in range(R):
+                nc.tensor.transpose(tps[h, j][:, i * P : (i + 1) * P], p[h, i][:, j * P : (j + 1) * P], ident[:])
+
+        def colsum(h, j):
+            if (h, j) in [(2, 0),(2, 2)]:
+                nc.vector.tensor_reduce(
+                    out=pcol[:, h * R + j : h * R + j + 1], in_=tps[h, j][:], axis=AX.X, op=ALU.add
+                )
+                return
+            nc.scalar.activation(
+                out=junk[j % 2][:], in_=tps[h, j][:], func=ACT.Copy, accum_out=pcol[:, h * R + j : h * R + j + 1]
+            )
+
+        def turn_last(i):
+            tps[H - 1, i] = bank(f"tl{i}", "t", (P, R, P))
+            for j in range(R):
+                nc.tensor.transpose(tps[H - 1, i][:, j, :], p[H - 1, i][:, j * P : (j + 1) * P], ident[:])
+
+        def colsum_last(i):
+            tp = tps[H - 1, i]
+            if i in [1,3]:
+                nc.vector.tensor_reduce(out=plast[:, :, i], in_=tp[:], axis=AX.X, op=ALU.add)
+            else:
+                for j in range(R):
+                    nc.scalar.activation(
+                        out=junk[i % 2][:, j * P : (j + 1) * P], in_=tp[:, j, :], func=ACT.Copy,
+                        accum_out=plast[:, j, i : i + 1],
+                    )
+
+        def split(lo, hi):
+            n = hi - lo
+            wide = [P, R, n]
+            if hi == H:
+                nc.vector.tensor_reduce(out=pcol[:, (H - 1) * R :], in_=plast[:], axis=AX.X, op=ALU.add)
+            pc = pcol[:, lo * R : hi * R].rearrange("p (h j) -> p j h", j=R)
+            u = sb(f"u{lo}", wide, F32)
+            v = sb(f"v{lo}", wide, F32)
+            if n == 1:
+                nc.vector.tensor_scalar(
+                    out=u[:], in0=pc, scalar1=w_inv[:, lo:hi], scalar2=1.0, op0=ALU.mult, op1=ALU.add
+                )
+                nc.vector.tensor_scalar(
+                    out=v[:], in0=pc, scalar1=w_pos[:, lo:hi], scalar2=-0.5 / N, op0=ALU.add, op1=ALU.mult
+                )
+            else:
+                nc.vector.tensor_tensor(
+                    out=u[:], in0=pc, in1=w_inv[:, lo:hi].unsqueeze(1).to_broadcast(wide), op=ALU.mult
+                )
+                nc.vector.tensor_tensor(
+                    out=v[:], in0=pc, in1=w_pos[:, lo:hi].unsqueeze(1).to_broadcast(wide), op=ALU.add
+                )
+                nc.vector.tensor_scalar(out=u[:], in0=u[:], scalar1=1.0, scalar2=None, op0=ALU.add)
+                nc.vector.tensor_scalar(out=v[:], in0=v[:], scalar1=-0.5 / N, scalar2=None, op0=ALU.mult)
+            left = [u, v]
+            for lev in range(3):
+                got = []
+                for k in range(2):
+                    rows = uvt[k][:, :, 0 : 9 * H].rearrange("p j (a c h) -> p j a c h", a=3, c=3)
+                    dst = rows[:, :, lev, :, lo:hi] if k == 0 else rows[:, :, :, lev, lo:hi]
+                    nc.vector.tensor_copy(out=dst, in_=left[k][:].unsqueeze(2).to_broadcast([P, R, 3, n]))
+                    got.append(dst[:, :, 0, :])
+                if lev < 2:
+                    for k in range(2):
+                        rest = sb(f"rest{lo}{k}{lev}", wide, F32)
+                        nc.vector.tensor_tensor(out=rest[:], in0=left[k][:], in1=got[k], op=ALU.subtract)
+                        left[k] = rest
+
+        def consts():
+            nc.vector.tensor_scalar(out=w_pos[:], in0=w_bf[:], scalar1=float(N), scalar2=None, op0=ALU.mult)
+            nc.vector.tensor_copy(out=bias[:], in_=b_bf[:])
+            nc.vector.tensor_scalar(out=w_inv[:], in0=w_pos[:], scalar1=0.0, scalar2=None, op0=ALU.is_equal)
+            nc.vector.tensor_tensor(out=w_inv[:], in0=w_inv[:], in1=w_pos[:], op=ALU.add)
+            nc.vector.reciprocal(w_inv[:], w_inv[:])
+
+        gts = {}
+
+        def turn_gain():
+            gts[0] = psum.tile([P, P], BF16, name="gt", tag="t", bufs=BUFS["t"])
+            nc.tensor.transpose(gts[0][:], g_rows[:], ident16[:])
+
+        def copy_gain():
+            nc.vector.tensor_copy(out=gain[:].rearrange("p h t -> p (h t)"), in_=gts[0][:, 0 : H * T])
+
+        zs = {}
+
+        def turn_rt():
+            zs["u"] = bank("rt", "l", dtype=BF16)
+            for j in range(R):
+                nc.tensor.transpose(zs["u"][:, j * P : (j + 1) * P], uvt[0][:, j, :], ident16[:])
+
+        def turn_vt():
+            zs["v"] = bank("vt", "l", dtype=BF16)
+            for j in range(R):
+                nc.tensor.transpose(zs["v"][:, j * P : (j + 1) * P], uvt[1][:, j, :], ident16[:])
+
+        def copy_rt():
+            nc.scalar.copy(out=ru[:], in_=zs["u"][:])
+
+        def copy_vt():
+            nc.vector.tensor_copy(out=rv[:], in_=zs["v"][:])
+
+        def turn_acc(i):
+            zs[i] = bank(f"z{i}", ["p","p","p","l"][i])
+            for j in range(R):
+                nc.tensor.matmul(
+                    zs[i][:, j * P : (j + 1) * P], lhsT=acc[j][:, i * P : (i + 1) * P], rhs=ident[:],
+                    is_transpose=True, start=(j == 0), stop=False,
+                )
+
+        def outer(i):
+            nc.tensor.matmul(zs[i][:], lhsT=ru[:, i * P : (i + 1) * P], rhs=rv[:], start=False, stop=True)
+
+        def combine(i):
+            nc.vector.tensor_tensor(out=res[i][:], in0=zs[i][:], in1=acc[i][:], op=ALU.add)
+
+        def sigmoid(i):
+            nc.scalar.activation(out=osb[i][:], in_=res[i][:], func=ACT.Sigmoid, bias=bias[:])
+
+        def store(i):
+            nc.sync.dma_start(out=out[i * P : (i + 1) * P, :], in_=osb[i][:])
+
+        mult_x(0)
+        turn_x(0)
+        pack_x(0)
+        mult_x(1)
+        turn_x(1)
+        pack_x(1)
+        perm_s("k")
+        perm_w("k", 0)
+        quant_x(0)
+        proj("k", 1, 0)
+        mult_x(2)
+        empty("k", 1, 0)
+        proj("k", 0, 0)
+        turn_x(2)
+        empty("k", 0, 0)
+        quant_x(1)
+        mult_x(3)
+        pack_x(2)
+        turn_gain()
+        proj("k", 0, 1)
+        copy_gain()
+        perm_s("q")
+        quant_x(2)
+        proj("k", 1, 1)
+        empty("k", 0, 1)
+        empty("k", 1, 1)
+        turn_x(3)
+        pack_x(3)
+        proj("k", 0, 2)
+        empty("k", 0, 2)
+        proj("k", 1, 2)
+        empty("k", 1, 2)
+        perm_w("k", 1)
+        perm_w("q", 0)
+        proj("q", 0, 0)
+        proj("q", 0, 1)
+        perm_w("q", 1)
+        quant_x(3)
+        empty("q", 0, 0)
+        proj("k", 0, 3)
+        proj("k", 1, 3)
+        empty("k", 0, 3)
+        empty("q", 0, 1)
+        quant("q", 0, 0, 256)
+        empty("k", 1, 3)
+        proj("q", 0, 3)
+        quant("k", 0, 0, N)
+        proj("q", 0, 2)
+        empty("q", 0, 3)
+        empty("q", 0, 2)
+        proj("q", 1, 0)
+        empty("q", 1, 0)
+        score(0, 1)
+        row_max(0, 1)
+        negate(0, 1)
+        expo(0, 1)
+        proj("q", 1, 1)
+        empty("q", 1, 1)
+        proj("k", 2, 0)
+        empty("k", 2, 0)
+        quant("q", 0, 256, N)
+        score(0, 0)
+        row_max(0, 0)
+        proj("q", 1, 2)
+        score(0, 2)
+        negate(0, 0)
+        expo(0, 0)
+        consts()
+        empty("q", 1, 2)
+        row_max(0, 2)
+        proj("k", 2, 1)
+        empty("k", 2, 1)
+        negate(0, 2)
+        quant("q", 1, 0, 256)
+        recip(0, 0)
+        proj("q", 2, 0)
+        recip(0, 1)
+        score(0, 3)
+        empty("q", 2, 0)
+        quant("k", 1, 0, N)
+        proj("k", 2, 2)
+        expo(0, 2)
+        recip(0, 2)
+        empty("k", 2, 2)
+        weigh(0, 0)
+        proj("q", 1, 3)
+        proj("k", 2, 3)
+        empty("k", 2, 3)
+        empty("q", 1, 3)
+        row_max(0, 3)
+        proj("q", 2, 1)
+        empty("q", 2, 1)
+        negate(0, 3)
+        expo(0, 3)
+        score(1, 0)
+        row_max(1, 0)
+        score(1, 1)
+        quant("q", 1, 256, N)
+        negate(1, 0)
+        expo(1, 0)
+        proj("q", 2, 2)
+        weigh(0, 1)
+        recip(0, 3)
+        empty("q", 2, 2)
+        proj("k", 3, 1)
+        empty("k", 3, 1)
+        proj("k", 3, 0)
+        row_max(1, 1)
+        negate(1, 1)
+        empty("k", 3, 0)
+        recip(1, 0)
+        weigh(0, 3)
+        score(1, 3)
+        proj("q", 2, 3)
+        row_max(1, 3)
+        quant("q", 2, 0, 256)
+        score(1, 2)
+        weigh(0, 2)
+        turn_p(0, 1)
+        row_max(1, 2)
+        proj("k", 3, 3)
+        empty("q", 2, 3)
+        turn_p(0, 0)
+        negate(1, 3)
+        expo(1, 1)
+        weigh(1, 0)
+        recip(1, 1)
+        proj("q", 3, 0)
+        expo(1, 3)
+        gather(1, 0)
+        weigh(1, 1)
+        quant("k", 2, 0, N)
+        negate(1, 2)
+        recip(1, 3)
+        quant("q", 2, 256, N)
+        proj("q", 3, 1)
+        empty("k", 3, 3)
+        expo(1, 2)
+        score(2, 0)
+        empty("q", 3, 0)
+        gather(1, 1)
+        colsum(0, 1)
+        recip(1, 2)
+        row_max(2, 0)
+        colsum(0, 0)
+        weigh(1, 2)
+        empty("q", 3, 1)
+        weigh(1, 3)
+        score(2, 1)
+        row_max(2, 1)
+        proj("k", 3, 2)
+        negate(2, 0)
+        empty("k", 3, 2)
+        expo(2, 0)
+        negate(2, 1)
+        score(2, 2)
+        gather(1, 2)
+        row_max(2, 2)
+        turn_p(0, 2)
+        turn_p(0, 3)
+        proj("q", 3, 3)
+        recip(2, 0)
+        quant("q", 3, 0, 256)
+        colsum(0, 2)
+        proj("q", 3, 2)
+        quant("k", 3, 0, N)
+        negate(2, 2)
+        score(2, 3)
+        row_max(2, 3)
+        expo(2, 1)
+        colsum(0, 3)
+        empty("q", 3, 3)
+        turn_p(1, 1)
+        negate(2, 3)
+        expo(2, 2)
+        score(3, 0)
+        gather(1, 3)
+        row_max(3, 0)
+        recip(2, 1)
+        recip(2, 2)
+        expo(2, 3)
+        weigh(2, 0)
+        negate(3, 0)
+        score(3, 1)
+        empty("q", 3, 2)
+        turn_p(1, 0)
+        weigh(2, 2)
+        row_max(3, 1)
+        quant("q", 3, 256, N)
+        score(3, 3)
+        colsum(1, 1)
+        weigh(2, 1)
+        recip(2, 3)
+        expo(3, 0)
+        recip(3, 0)
+        negate(3, 1)
+        expo(3, 1)
+        weigh(3, 0)
+        score(3, 2)
+        turn_last(0)
+        weigh(2, 3)
+        turn_p(2, 0)
+        colsum(1, 0)
+        row_max(3, 3)
+        recip(3, 1)
+        turn_p(2, 1)
+        turn_p(2, 2)
+        row_max(3, 2)
+        gather(2, 1)
+        gather(2, 0)
+        negate(3, 3)
+        weigh(3, 1)
+        turn_last(1)
+        colsum_last(0)
+        turn_p(1, 2)
+        gather(2, 3)
+        negate(3, 2)
+        colsum(2, 0)
+        expo(3, 3)
+        colsum_last(1)
+        expo(3, 2)
+        turn_p(2, 3)
+        colsum(1, 2)
+        turn_p(1, 3)
+        gather(2, 2)
+        colsum(1, 3)
+        recip(3, 3)
+        recip(3, 2)
+        colsum(2, 1)
+        weigh(3, 2)
+        turn_last(2)
+        weigh(3, 3)
+        gather(3, 3)
+        colsum_last(2)
+        gather(3, 0)
+        colsum(2, 2)
+        colsum(2, 3)
+        turn_last(3)
+        gather(3, 1)
+        colsum_last(3)
+        split(0, 4)
+        turn_rt()
+        turn_vt()
+        gather(3, 2)
+        turn_acc(3)
+        turn_acc(0)
+        turn_acc(1)
+        copy_rt()
+        copy_vt()
+        outer(0)
+        combine(0)
+        outer(1)
+        sigmoid(0)
+        store(0)
+        turn_acc(2)
+        outer(2)
+        combine(1)
+        sigmoid(1)
+        store(1)
+        combine(2)
+        outer(3)
+        sigmoid(2)
+        store(2)
+        combine(3)
+        sigmoid(3)
+        store(3)

@@ -44,7 +44,7 @@ def tile_esmcontactheadapc_w4_kernel(
             return psum.tile(list(shape), dtype, name=name, tag=tag, bufs=BUFS[tag])
 
         xb = [sb(f"xb{i}", [P, D], U8) for i in range(R)]
-        xscale = sb("xscale", [P, D], F32)
+        xscale = sb("xscale", [P, G, T], F32)
         xs = [sb(f"xs{i}", [P, D], BF16) for i in range(R)]
         xg = [sb(f"xg{i}", [P, G, P, T], BF16) for i in range(R)]
         xc = sb("xc", [P, G, N], U32)
@@ -109,12 +109,12 @@ def tile_esmcontactheadapc_w4_kernel(
         nc.gpsimd.memset(uvt[0][:], 0.0)
         nc.gpsimd.memset(uvt[1][:], 0.0)
 
-        nc.scalar.dma_start(out=xscale[:], in_=x_scale.rearrange("o k -> (o k)").partition_broadcast(P))
+        nc.scalar.dma_start(out=xscale[:], in_=x_scale.rearrange("o (g p t) -> p (o g) t", g=G, t=T))
         nc.scalar.activation(out=dummy[:], in_=zero[:], func=ACT.Exp)
         load_x(0)
-        load_x(1)
-        load_w("k", 0)
         load_s("k")
+        load_w("k", 0)
+        load_x(1)
         load_x(2)
         load_x(3)
         load_s("q")
@@ -130,8 +130,11 @@ def tile_esmcontactheadapc_w4_kernel(
         nc.scalar.dma_start(out=b_bf[:], in_=b_head.partition_broadcast(P))
         nc.vector.tensor_copy(out=ident16[:], in_=ident[:])
 
-        def mult_x(i):
-            nc.vector.tensor_tensor(out=xs[i][:], in0=xb[i][:].bitcast(FP8), in1=xscale[:], op=ALU.mult)
+        def widen_x(i):
+            if i in [0]:
+                nc.vector.tensor_copy(out=xs[i][:], in_=xb[i][:].bitcast(FP8))
+            else:
+                nc.scalar.copy(out=xs[i][:], in_=xb[i][:].bitcast(FP8))
 
         xts = {}
 
@@ -142,8 +145,14 @@ def tile_esmcontactheadapc_w4_kernel(
                 for u in range(2):
                     nc.tensor.transpose(xts[i][:, g, u, :], w[:, 256 * g + u : 256 * (g + 1) : 2], ident[:])
 
-        def pack_x(i):
-            nc.scalar.copy(out=xg[i][:].bitcast(F32), in_=xts[i][:].rearrange("p g u r -> p g r u"))
+        def scale_x(i):
+            for g in range(G):
+                nc.vector.tensor_tensor(
+                    out=xg[i][:, g].rearrange("p r (u e) -> p r u e", u=2),
+                    in0=xts[i][:, g].bitcast(BF16).rearrange("p u (r e) -> p r u e", e=2),
+                    in1=xscale[:, g : g + 1, :].to_broadcast([P, P, T]).rearrange("p r (u e) -> p r u e", u=2),
+                    op=ALU.mult,
+                )
 
         def quant_x(i):
             for g in range(G):
@@ -251,16 +260,24 @@ def tile_esmcontactheadapc_w4_kernel(
 
         def weigh(h, i):
             c = h * R + i
-            eng = nc.gpsimd if h < H - 1 else nc.vector
-            eng.tensor_scalar(
-                out=p[h, i][:], in0=e[h, i][:], scalar1=rinv[:, c : c + 1], scalar2=w_pos[:, h : h + 1],
-                op0=ALU.mult, op1=ALU.mult,
-            )
+            on_vector = (h, i) in [(3, 0),(3, 1),(3, 2),(3, 3)]
+            eng = nc.vector if on_vector else nc.gpsimd
+            n = 1 if on_vector else 1
+            for k in range(n):
+                cols = slice(k * N // n, (k + 1) * N // n)
+                eng.tensor_scalar(
+                    out=p[h, i][:, cols], in0=e[h, i][:, cols], scalar1=rinv[:, c : c + 1],
+                    scalar2=w_pos[:, h : h + 1], op0=ALU.mult, op1=ALU.mult,
+                )
 
         def gather(h, i):
-            eng = nc.vector if (h, i) in [(3, 3),(3, 2)] else nc.gpsimd
+            on_vector = (h, i) in [(3, 3),(3, 2)]
+            eng = nc.vector if on_vector else nc.gpsimd
             first = p[0, i] if h == 1 else acc[i]
-            eng.tensor_tensor(out=acc[i][:], in0=first[:], in1=p[h, i][:], op=ALU.add)
+            n = 1 if on_vector else 1
+            for k in range(n):
+                cols = slice(k * N // n, (k + 1) * N // n)
+                eng.tensor_tensor(out=acc[i][:, cols], in0=first[:, cols], in1=p[h, i][:, cols], op=ALU.add)
 
         tps = {}
 
@@ -387,269 +404,269 @@ def tile_esmcontactheadapc_w4_kernel(
         def store(i):
             nc.sync.dma_start(out=out[i * P : (i + 1) * P, :], in_=osb[i][:])
 
-        mult_x(0)
-        turn_x(0)
-        pack_x(0)
-        mult_x(1)
-        turn_x(1)
-        pack_x(1)
-        perm_s("k")
+        widen_x(0)
         perm_w("k", 0)
+        turn_x(0)
+        scale_x(0)
+        widen_x(2)
+        perm_s("k")
+        widen_x(3)
+        turn_x(2)
+        turn_x(3)
         quant_x(0)
         proj("k", 1, 0)
-        mult_x(2)
-        empty("k", 1, 0)
-        proj("k", 0, 0)
-        turn_x(2)
-        empty("k", 0, 0)
-        quant_x(1)
-        mult_x(3)
-        pack_x(2)
-        turn_gain()
-        proj("k", 0, 1)
-        copy_gain()
-        perm_s("q")
+        scale_x(2)
+        widen_x(1)
+        turn_x(1)
         quant_x(2)
-        proj("k", 1, 1)
-        empty("k", 0, 1)
-        empty("k", 1, 1)
-        turn_x(3)
-        pack_x(3)
-        proj("k", 0, 2)
-        empty("k", 0, 2)
+        scale_x(3)
+        turn_gain()
+        perm_s("q")
+        copy_gain()
         proj("k", 1, 2)
-        empty("k", 1, 2)
-        perm_w("k", 1)
-        perm_w("q", 0)
-        proj("q", 0, 0)
-        proj("q", 0, 1)
-        perm_w("q", 1)
+        proj("k", 0, 2)
         quant_x(3)
-        empty("q", 0, 0)
+        empty("k", 1, 0)
+        empty("k", 1, 2)
+        perm_w("q", 0)
+        empty("k", 0, 2)
+        proj("k", 0, 0)
+        empty("k", 0, 0)
+        scale_x(1)
         proj("k", 0, 3)
-        proj("k", 1, 3)
         empty("k", 0, 3)
-        empty("q", 0, 1)
-        quant("q", 0, 0, 256)
-        empty("k", 1, 3)
+        quant_x(1)
         proj("q", 0, 3)
-        quant("k", 0, 0, N)
         proj("q", 0, 2)
+        proj("k", 0, 1)
         empty("q", 0, 3)
         empty("q", 0, 2)
-        proj("q", 1, 0)
-        empty("q", 1, 0)
-        score(0, 1)
-        row_max(0, 1)
-        negate(0, 1)
-        expo(0, 1)
-        proj("q", 1, 1)
-        empty("q", 1, 1)
+        perm_w("k", 1)
+        proj("q", 0, 1)
+        proj("k", 1, 3)
+        empty("k", 0, 1)
+        empty("q", 0, 1)
         proj("k", 2, 0)
-        empty("k", 2, 0)
+        quant("k", 0, 0, N)
+        proj("q", 0, 0)
         quant("q", 0, 256, N)
-        score(0, 0)
-        row_max(0, 0)
-        proj("q", 1, 2)
+        empty("k", 1, 3)
+        perm_w("q", 1)
+        score(0, 3)
+        empty("q", 0, 0)
+        proj("k", 2, 2)
+        empty("k", 2, 0)
         score(0, 2)
+        empty("k", 2, 2)
+        proj("q", 2, 2)
+        row_max(0, 3)
+        proj("k", 1, 1)
+        proj("k", 2, 1)
+        row_max(0, 2)
+        negate(0, 3)
+        quant("q", 0, 0, 256)
+        expo(0, 3)
+        negate(0, 2)
+        score(0, 0)
+        empty("q", 2, 2)
+        proj("q", 1, 2)
+        empty("k", 1, 1)
+        expo(0, 2)
+        empty("k", 2, 1)
+        recip(0, 3)
+        consts()
+        row_max(0, 0)
+        proj("q", 1, 3)
+        recip(0, 2)
+        score(0, 1)
+        empty("q", 1, 2)
+        empty("q", 1, 3)
         negate(0, 0)
         expo(0, 0)
-        consts()
-        empty("q", 1, 2)
-        row_max(0, 2)
-        proj("k", 2, 1)
-        empty("k", 2, 1)
-        negate(0, 2)
-        quant("q", 1, 0, 256)
-        recip(0, 0)
-        proj("q", 2, 0)
-        recip(0, 1)
-        score(0, 3)
-        empty("q", 2, 0)
-        quant("k", 1, 0, N)
-        proj("k", 2, 2)
-        expo(0, 2)
-        recip(0, 2)
-        empty("k", 2, 2)
-        weigh(0, 0)
-        proj("q", 1, 3)
+        row_max(0, 1)
+        proj("k", 3, 3)
         proj("k", 2, 3)
+        empty("k", 3, 3)
+        quant("q", 1, 256, N)
+        negate(0, 1)
+        proj("q", 1, 1)
+        recip(0, 0)
+        quant("k", 1, 0, N)
         empty("k", 2, 3)
-        empty("q", 1, 3)
-        row_max(0, 3)
-        proj("q", 2, 1)
-        empty("q", 2, 1)
-        negate(0, 3)
-        expo(0, 3)
+        empty("q", 1, 1)
+        proj("q", 2, 3)
+        proj("q", 1, 0)
+        expo(0, 1)
+        score(1, 3)
+        weigh(0, 2)
+        empty("q", 2, 3)
+        recip(0, 1)
+        weigh(0, 3)
+        proj("k", 3, 2)
+        empty("k", 3, 2)
+        empty("q", 1, 0)
+        weigh(0, 0)
+        row_max(1, 3)
+        quant("q", 1, 0, 256)
+        score(1, 2)
+        row_max(1, 2)
+        weigh(0, 1)
+        negate(1, 3)
+        quant("q", 2, 256, N)
+        expo(1, 3)
+        proj("k", 3, 1)
+        turn_p(0, 0)
+        negate(1, 2)
+        colsum(0, 0)
+        recip(1, 3)
+        expo(1, 2)
+        quant("k", 2, 0, N)
         score(1, 0)
         row_max(1, 0)
-        score(1, 1)
-        quant("q", 1, 256, N)
+        proj("q", 2, 0)
         negate(1, 0)
-        expo(1, 0)
-        proj("q", 2, 2)
-        weigh(0, 1)
-        recip(0, 3)
-        empty("q", 2, 2)
-        proj("k", 3, 1)
-        empty("k", 3, 1)
-        proj("k", 3, 0)
-        row_max(1, 1)
-        negate(1, 1)
-        empty("k", 3, 0)
-        recip(1, 0)
-        weigh(0, 3)
-        score(1, 3)
-        proj("q", 2, 3)
-        row_max(1, 3)
-        quant("q", 2, 0, 256)
-        score(1, 2)
-        weigh(0, 2)
-        turn_p(0, 1)
-        row_max(1, 2)
-        proj("k", 3, 3)
-        empty("q", 2, 3)
-        turn_p(0, 0)
-        negate(1, 3)
-        expo(1, 1)
-        weigh(1, 0)
-        recip(1, 1)
-        proj("q", 3, 0)
-        expo(1, 3)
-        gather(1, 0)
-        weigh(1, 1)
-        quant("k", 2, 0, N)
-        negate(1, 2)
-        recip(1, 3)
-        quant("q", 2, 256, N)
-        proj("q", 3, 1)
-        empty("k", 3, 3)
-        expo(1, 2)
-        score(2, 0)
-        empty("q", 3, 0)
-        gather(1, 1)
-        colsum(0, 1)
+        proj("q", 2, 1)
         recip(1, 2)
-        row_max(2, 0)
-        colsum(0, 0)
-        weigh(1, 2)
-        empty("q", 3, 1)
-        weigh(1, 3)
-        score(2, 1)
-        row_max(2, 1)
-        proj("k", 3, 2)
-        negate(2, 0)
-        empty("k", 3, 2)
-        expo(2, 0)
-        negate(2, 1)
-        score(2, 2)
-        gather(1, 2)
-        row_max(2, 2)
-        turn_p(0, 2)
-        turn_p(0, 3)
-        proj("q", 3, 3)
-        recip(2, 0)
-        quant("q", 3, 0, 256)
-        colsum(0, 2)
-        proj("q", 3, 2)
-        quant("k", 3, 0, N)
-        negate(2, 2)
+        empty("k", 3, 1)
         score(2, 3)
+        weigh(1, 3)
+        score(1, 1)
+        turn_p(0, 1)
+        expo(1, 0)
+        proj("q", 3, 2)
+        score(2, 2)
+        empty("q", 2, 0)
         row_max(2, 3)
-        expo(2, 1)
-        colsum(0, 3)
-        empty("q", 3, 3)
-        turn_p(1, 1)
+        proj("q", 3, 3)
+        row_max(1, 1)
         negate(2, 3)
-        expo(2, 2)
-        score(3, 0)
-        gather(1, 3)
-        row_max(3, 0)
-        recip(2, 1)
-        recip(2, 2)
         expo(2, 3)
-        weigh(2, 0)
-        negate(3, 0)
-        score(3, 1)
-        empty("q", 3, 2)
-        turn_p(1, 0)
-        weigh(2, 2)
-        row_max(3, 1)
-        quant("q", 3, 256, N)
-        score(3, 3)
-        colsum(1, 1)
-        weigh(2, 1)
+        empty("q", 2, 1)
+        weigh(1, 2)
+        proj("k", 3, 0)
+        negate(1, 1)
+        recip(1, 0)
+        turn_p(0, 3)
         recip(2, 3)
-        expo(3, 0)
-        recip(3, 0)
-        negate(3, 1)
-        expo(3, 1)
-        weigh(3, 0)
-        score(3, 2)
-        turn_last(0)
+        expo(1, 1)
+        empty("q", 3, 2)
+        quant("q", 2, 0, 256)
+        colsum(0, 1)
+        gather(1, 3)
+        recip(1, 1)
+        gather(1, 2)
         weigh(2, 3)
-        turn_p(2, 0)
-        colsum(1, 0)
-        row_max(3, 3)
-        recip(3, 1)
-        turn_p(2, 1)
-        turn_p(2, 2)
-        row_max(3, 2)
-        gather(2, 1)
-        gather(2, 0)
-        negate(3, 3)
-        weigh(3, 1)
-        turn_last(1)
-        colsum_last(0)
-        turn_p(1, 2)
+        empty("k", 3, 0)
+        weigh(1, 1)
+        row_max(2, 2)
+        score(2, 0)
+        negate(2, 2)
+        weigh(1, 0)
+        empty("q", 3, 3)
+        expo(2, 2)
+        colsum(0, 3)
+        row_max(2, 0)
+        negate(2, 0)
+        score(2, 1)
+        quant("q", 3, 256, N)
+        proj("q", 3, 0)
+        turn_p(1, 1)
+        quant("k", 3, 0, N)
+        expo(2, 0)
         gather(2, 3)
-        negate(3, 2)
-        colsum(2, 0)
-        expo(3, 3)
-        colsum_last(1)
-        expo(3, 2)
-        turn_p(2, 3)
-        colsum(1, 2)
+        colsum(1, 1)
         turn_p(1, 3)
-        gather(2, 2)
+        row_max(2, 1)
+        recip(2, 0)
+        score(3, 3)
+        recip(2, 2)
+        row_max(3, 3)
+        score(3, 2)
+        negate(2, 1)
+        proj("q", 3, 1)
+        weigh(2, 2)
+        empty("q", 3, 0)
+        empty("q", 3, 1)
+        expo(2, 1)
+        gather(1, 0)
+        turn_p(0, 2)
+        recip(2, 1)
         colsum(1, 3)
+        turn_p(1, 0)
+        quant("q", 3, 0, 256)
+        gather(1, 1)
+        negate(3, 3)
+        colsum(0, 2)
+        row_max(3, 2)
+        expo(3, 3)
+        score(3, 0)
+        row_max(3, 0)
+        weigh(2, 1)
+        weigh(2, 0)
         recip(3, 3)
-        recip(3, 2)
-        colsum(2, 1)
-        weigh(3, 2)
-        turn_last(2)
+        score(3, 1)
+        row_max(3, 1)
+        turn_p(2, 2)
+        colsum(1, 0)
+        negate(3, 0)
+        expo(3, 0)
+        negate(3, 2)
+        negate(3, 1)
         weigh(3, 3)
-        gather(3, 3)
-        colsum_last(2)
-        gather(3, 0)
-        colsum(2, 2)
-        colsum(2, 3)
+        turn_p(2, 1)
+        expo(3, 1)
+        recip(3, 0)
+        weigh(3, 0)
         turn_last(3)
-        gather(3, 1)
+        colsum(2, 2)
+        turn_last(0)
+        turn_p(2, 3)
+        recip(3, 1)
+        turn_p(2, 0)
+        expo(3, 2)
         colsum_last(3)
+        colsum(2, 1)
+        recip(3, 2)
+        weigh(3, 1)
+        turn_p(1, 2)
+        weigh(3, 2)
+        colsum_last(0)
+        colsum(1, 2)
+        turn_last(2)
+        colsum_last(2)
+        gather(3, 3)
+        turn_last(1)
+        colsum(2, 0)
+        colsum_last(1)
+        colsum(2, 3)
         split(0, 4)
         turn_rt()
-        turn_vt()
+        gather(2, 1)
+        gather(2, 2)
+        copy_rt()
+        gather(2, 0)
         gather(3, 2)
+        turn_vt()
+        gather(3, 1)
+        gather(3, 0)
+        turn_acc(2)
         turn_acc(3)
         turn_acc(0)
-        turn_acc(1)
-        copy_rt()
         copy_vt()
+        outer(2)
+        combine(2)
+        sigmoid(2)
         outer(0)
+        store(2)
+        turn_acc(1)
         combine(0)
+        outer(3)
+        combine(3)
         outer(1)
         sigmoid(0)
+        sigmoid(3)
         store(0)
-        turn_acc(2)
-        outer(2)
         combine(1)
         sigmoid(1)
-        store(1)
-        combine(2)
-        outer(3)
-        sigmoid(2)
-        store(2)
-        combine(3)
-        sigmoid(3)
         store(3)
+        store(1)

@@ -38,7 +38,7 @@ def tile_esmcontactheadapc_w4_kernel(
         def sb(name, shape, dtype, align=64):
             return keep.tile(shape, dtype, name=name, align_bytes=align)
 
-        BUFS = {"p": 3, "l": 3, "t": 2}
+        BUFS = {"p": 4, "l": 3, "t": 1}
 
         def bank(name, tag, shape=(P, 512), dtype=F32):
             return psum.tile(list(shape), dtype, name=name, tag=tag, bufs=BUFS[tag])
@@ -51,14 +51,14 @@ def tile_esmcontactheadapc_w4_kernel(
         xcs = sb("xcs", [P, G, N], U8)
         words = {"q": w_q_words, "k": w_k_words}
         scales = {"q": w_q_scales, "k": w_k_scales}
-        wraw = {(s, j): sb(f"wraw_{s}{j}", [P, G, 2048], U8) for s in "qk" for j in range(2)}
-        wp = {(s, j): sb(f"wp_{s}{j}", [P, T, G, 512], U8) for s in "qk" for j in range(2)}
+        wraw = {(s, h): sb(f"wraw_{s}{h}", [P, G, 2 * E], U8) for s in "qk" for h in range(H)}
+        wp = {(s, h): sb(f"wp_{s}{h}", [P, T, G, 2 * P], U8) for s in "qk" for h in range(H)}
         sraw = {s: sb(f"sraw_{s}", [P, G, H * E], U8) for s in "qk"}
         sp = {s: sb(f"sp_{s}", [P, T, G, H * P], U8) for s in "qk"}
         grp = {(s, h): sb(f"grp_{s}{h}", [P, N, T], BF16) for s in "qk" for h in range(H)}
         code = {(s, h): sb(f"code_{s}{h}", [P, N], U32) for s in "qk" for h in range(H)}
         cscl = {(s, h): sb(f"cscl_{s}{h}", [P, N], U8) for s in "qk" for h in range(H)}
-        flat = {h: sb(f"flat{h}", [P, T, N], BF16) for h in []}
+        flat = {h: sb(f"flat{h}", [P, T, N], BF16) for h in [2]}
         e = {(h, i): sb(f"e{h}{i}", [P, N], F32) for h in range(H) for i in range(R)}
         p = {(h, i): sb(f"p{h}{i}", [P, N], F32) for h in range(H) for i in range(R)}
         acc = [sb(f"acc{i}", [P, N], F32) for i in range(R)]
@@ -77,9 +77,12 @@ def tile_esmcontactheadapc_w4_kernel(
         rowmax = sb("rowmax", [P, S], F32)
         nbias = sb("nbias", [P, S], F32)
         rowsum = sb("rowsum", [P, S], F32)
+        cfac = sb("cfac", [P, S], F32)
         rinv = sb("rinv", [P, S], F32)
         pcol = sb("pcol", [P, S], F32)
-        plast = sb("plast", [P, R, R], F32)
+        rest = [sb(f"rest{k}", [P, R, H], F32) for k in range(2)]
+        u_all = sb("u_all", [P, R, H], F32)
+        v_all = sb("v_all", [P, R, H], F32)
         uvt = [sb(f"uvt{k}", [P, R, P], BF16) for k in range(2)]
         ru = sb("ru", [P, N], BF16)
         rv = sb("rv", [P, N], BF16)
@@ -89,9 +92,9 @@ def tile_esmcontactheadapc_w4_kernel(
         def load_x(i):
             nc.sync.dma_start(out=xb[i][:], in_=x_bytes[i * P : (i + 1) * P, :])
 
-        def load_w(s, j):
+        def load_w(s, h):
             nc.sync.dma_start(
-                out=wraw[s, j][:], in_=words[s][:, :, j * 2048 : (j + 1) * 2048].rearrange("g p c -> p g c")
+                out=wraw[s, h][:], in_=words[s][:, :, 2 * E * h : 2 * E * (h + 1)].rearrange("g p c -> p g c")
             )
 
         def load_s(s):
@@ -101,6 +104,11 @@ def tile_esmcontactheadapc_w4_kernel(
                     in_=scales[s].bitcast(I32)[:, 4 * q : 4 * q + 4, :].rearrange("g q n -> q g n"),
                 )
 
+        idle = sb("idle", [P, N], BF16)
+        nc.vector.memset(idle[:], 0.0)
+        wb = bank("warm", "l")
+        for k in range(4):
+            nc.tensor.matmul(wb[:], lhsT=idle[:, 0:P], rhs=idle[:], start=True, stop=True)
         nc.vector.memset(sraw["k"][:].rearrange("p g c -> p (g c)").bitcast(I32), 0)
         nc.vector.memset(zero[:], 0.0)
         nc.vector.memset(sraw["q"][:].rearrange("p g c -> p (g c)").bitcast(I32), 0)
@@ -115,12 +123,16 @@ def tile_esmcontactheadapc_w4_kernel(
         load_s("k")
         load_w("k", 0)
         load_x(1)
+        load_w("k", 1)
         load_x(2)
         load_x(3)
         load_s("q")
         load_w("q", 0)
-        load_w("k", 1)
         load_w("q", 1)
+        load_w("k", 2)
+        load_w("q", 2)
+        load_w("k", 3)
+        load_w("q", 3)
         for h in range(H):
             nc.scalar.dma_start(
                 out=g_rows[T * h : T * (h + 1), :].rearrange("t (b i) -> t b i", i=8),
@@ -128,7 +140,6 @@ def tile_esmcontactheadapc_w4_kernel(
             )
         nc.scalar.dma_start(out=w_bf[:], in_=w_head.partition_broadcast(P))
         nc.scalar.dma_start(out=b_bf[:], in_=b_head.partition_broadcast(P))
-        nc.vector.tensor_copy(out=ident16[:], in_=ident[:])
 
         def widen_x(i):
             if i in [0]:
@@ -161,24 +172,24 @@ def tile_esmcontactheadapc_w4_kernel(
                     out=xc[:, g, r].bitcast(FP8X4), scales=xcs[:, g, r], in_=xg[i][:, g].rearrange("p r t -> p (r t)")
                 )
 
-        def perm_w(s, j):
+        def perm_w(s, h):
             nc.vector.tensor_copy(
-                out=wp[s, j][:].rearrange("p t g c -> p t (g c)").bitcast(I32).rearrange("p t (b i) -> p t b i", i=4),
-                in_=wraw[s, j][:].rearrange("p g c -> p (g c)").bitcast(I32).rearrange("p (b t i) -> p t b i", t=T, i=4),
+                out=wp[s, h][:].rearrange("p t g c -> p t (g c)").bitcast(I32).rearrange("p t (b i) -> p t b i", i=4),
+                in_=wraw[s, h][:].rearrange("p g c -> p (g c)").bitcast(I32).rearrange("p (b t i) -> p t b i", t=T, i=4),
             )
 
-        def perm_s(s):
-            nc.vector.tensor_copy(
-                out=sp[s][:].rearrange("p t g c -> p t (g c)").bitcast(I32).rearrange("p t (b i) -> p t b i", i=2),
-                in_=sraw[s][:].rearrange("p g c -> p (g c)").bitcast(I32).rearrange("p (b t i) -> p t b i", t=T, i=2),
-            )
+        def perm_s(s, lo, hi):
+            for g in range(G):
+                nc.vector.tensor_copy(
+                    out=sp[s][:, :, g, P * lo : P * hi].bitcast(I32).rearrange("p t (b i) -> p t b i", i=2),
+                    in_=sraw[s][:, g, E * lo : E * hi].bitcast(I32).rearrange("p (b t i) -> p t b i", t=T, i=2),
+                )
 
         def mx(dst, s, h, t, lo, hi):
-            c = 256 * (h % 2)
             for g in range(G):
                 nc.tensor.matmul_mx(
                     out=dst,
-                    lhsT=wp[s, h // 2][:, t, g, c : c + 256].bitcast(FP4X4),
+                    lhsT=wp[s, h][:, t, g, :].bitcast(FP4X4),
                     lhsT_scale=sp[s][:, t, g, h * P : (h + 1) * P],
                     rhs=xc[:, g, lo:hi].bitcast(FP8X4),
                     rhs_scale=xcs[:, g, lo:hi],
@@ -214,7 +225,9 @@ def tile_esmcontactheadapc_w4_kernel(
         def weave(h, lo, hi):
             if h in flat:
                 src = flat[h][:, :, lo:hi].rearrange("p t n -> p n t")
-                nc.vector.tensor_copy(out=grp["q", h][:, lo:hi, :], in_=src)
+                nc.gpsimd.tensor_scalar(
+                    out=grp["q", h][:, lo:hi, :], in0=src, scalar1=1.0, scalar2=0.0, op0=ALU.mult, op1=ALU.add
+                )
 
         def quant(s, h, lo, hi):
             nc.vector.quantize_mx(
@@ -260,6 +273,12 @@ def tile_esmcontactheadapc_w4_kernel(
 
         def weigh(h, i):
             c = h * R + i
+            if (h, i) in []:
+                nc.vector.tensor_tensor(
+                    out=cfac[:, c : c + 1], in0=rinv[:, c : c + 1], in1=w_pos[:, h : h + 1], op=ALU.mult
+                )
+                nc.scalar.activation(out=p[h, i][:], in_=e[h, i][:], func=ACT.Copy, scale=cfac[:, c : c + 1])
+                return
             on_vector = (h, i) in [(3, 0),(3, 1),(3, 2),(3, 3)]
             eng = nc.vector if on_vector else nc.gpsimd
             n = 1 if on_vector else 1
@@ -270,94 +289,100 @@ def tile_esmcontactheadapc_w4_kernel(
                     scalar2=w_pos[:, h : h + 1], op0=ALU.mult, op1=ALU.mult,
                 )
 
-        def gather(h, i):
-            on_vector = (h, i) in [(3, 3),(3, 2)]
-            eng = nc.vector if on_vector else nc.gpsimd
-            first = p[0, i] if h == 1 else acc[i]
-            n = 1 if on_vector else 1
-            for k in range(n):
-                cols = slice(k * N // n, (k + 1) * N // n)
-                eng.tensor_tensor(out=acc[i][:, cols], in0=first[:, cols], in1=p[h, i][:, cols], op=ALU.add)
+        zs = {}
+        writes = [0] * R
+
+        def add_turned(j, h, i):
+            if j not in zs:
+                zs[j] = bank(f"z{j}", "p")
+            nc.tensor.matmul(
+                zs[j][:, i * P : (i + 1) * P], lhsT=p[h, i][:, j * P : (j + 1) * P], rhs=ident[:],
+                is_transpose=True, start=(writes[j] == 0), stop=(writes[j] == S - 1),
+            )
+            writes[j] += 1
+
+        def gather(j, h):
+            for i in range(R):
+                add_turned(j, h, i)
+
+        def gather_last(i):
+            for j in range(R):
+                add_turned(j, H - 1, i)
+
+        def keep_z(j):
+            if j in [0,1]:
+                nc.vector.tensor_copy(out=acc[j][:], in_=zs[j][:])
+            else:
+                nc.scalar.copy(out=acc[j][:], in_=zs[j][:])
 
         tps = {}
 
-        def turn_p(h, j):
-            tps[h, j] = bank(f"tp{h}{j}", "p" if h == H - 2 else "t")
-            for i in range(R):
-                nc.tensor.transpose(tps[h, j][:, i * P : (i + 1) * P], p[h, i][:, j * P : (j + 1) * P], ident[:])
+        turned = [0] * H
 
-        def colsum(h, j):
-            if (h, j) in [(2, 0),(2, 2)]:
-                nc.vector.tensor_reduce(
-                    out=pcol[:, h * R + j : h * R + j + 1], in_=tps[h, j][:], axis=AX.X, op=ALU.add
-                )
-                return
-            nc.scalar.activation(
-                out=junk[j % 2][:], in_=tps[h, j][:], func=ACT.Copy, accum_out=pcol[:, h * R + j : h * R + j + 1]
-            )
-
-        def turn_last(i):
-            tps[H - 1, i] = bank(f"tl{i}", "t", (P, R, P))
+        def turn_col(h, i):
+            if h not in tps:
+                tps[h] = bank(f"tp{h}", "t", (P, R, P))
             for j in range(R):
-                nc.tensor.transpose(tps[H - 1, i][:, j, :], p[H - 1, i][:, j * P : (j + 1) * P], ident[:])
+                nc.tensor.matmul(
+                    tps[h][:, j, :], lhsT=p[h, i][:, j * P : (j + 1) * P], rhs=ident[:], is_transpose=True,
+                    start=(turned[h] == 0), stop=(turned[h] == S - 1),
+                )
+                turned[h] += 1
 
-        def colsum_last(i):
-            tp = tps[H - 1, i]
-            if i in [1,3]:
-                nc.vector.tensor_reduce(out=plast[:, :, i], in_=tp[:], axis=AX.X, op=ALU.add)
-            else:
+        def colsum(h):
+            if h in [0,1,2]:
                 for j in range(R):
                     nc.scalar.activation(
-                        out=junk[i % 2][:, j * P : (j + 1) * P], in_=tp[:, j, :], func=ACT.Copy,
-                        accum_out=plast[:, j, i : i + 1],
+                        out=junk[h % 2][:, j * P : (j + 1) * P], in_=tps[h][:, j, :], func=ACT.Copy,
+                        accum_out=pcol[:, h * R + j : h * R + j + 1],
                     )
-
-        def split(lo, hi):
-            n = hi - lo
-            wide = [P, R, n]
-            if hi == H:
-                nc.vector.tensor_reduce(out=pcol[:, (H - 1) * R :], in_=plast[:], axis=AX.X, op=ALU.add)
-            pc = pcol[:, lo * R : hi * R].rearrange("p (h j) -> p j h", j=R)
-            u = sb(f"u{lo}", wide, F32)
-            v = sb(f"v{lo}", wide, F32)
-            if n == 1:
-                nc.vector.tensor_scalar(
-                    out=u[:], in0=pc, scalar1=w_inv[:, lo:hi], scalar2=1.0, op0=ALU.mult, op1=ALU.add
-                )
-                nc.vector.tensor_scalar(
-                    out=v[:], in0=pc, scalar1=w_pos[:, lo:hi], scalar2=-0.5 / N, op0=ALU.add, op1=ALU.mult
-                )
             else:
+                nc.vector.tensor_reduce(out=pcol[:, h * R : (h + 1) * R], in_=tps[h][:], axis=AX.X, op=ALU.add)
+
+        def uv(h):
+            pc = pcol[:, h * R : (h + 1) * R]
+            nc.vector.tensor_scalar(
+                out=u_all[:, :, h], in0=pc, scalar1=w_inv[:, h : h + 1], scalar2=1.0, op0=ALU.mult, op1=ALU.add
+            )
+            nc.vector.tensor_scalar(
+                out=v_all[:, :, h], in0=pc, scalar1=w_pos[:, h : h + 1], scalar2=-0.5 / N, op0=ALU.add, op1=ALU.mult
+            )
+
+        def rows(k, lev):
+            cells = uvt[k][:, :, 0 : 9 * H].rearrange("p j (a c h) -> p j a c h", a=3, c=3)
+            return cells[:, :, lev, :, :] if k == 0 else cells[:, :, :, lev, :]
+
+        def split():
+            thrice = [P, R, 3, H]
+            whole = [u_all, v_all]
+            for k in range(2):
+                nc.vector.tensor_copy(out=rows(k, 0), in_=whole[k][:].unsqueeze(2).to_broadcast(thrice))
+            for k in range(2):
+                nc.vector.tensor_tensor(out=rest[k][:], in0=whole[k][:], in1=rows(k, 0)[:, :, 0, :], op=ALU.subtract)
+            for k in range(2):
                 nc.vector.tensor_tensor(
-                    out=u[:], in0=pc, in1=w_inv[:, lo:hi].unsqueeze(1).to_broadcast(wide), op=ALU.mult
+                    out=rows(k, 1), in0=whole[k][:].unsqueeze(2).to_broadcast(thrice), in1=rows(k, 0), op=ALU.subtract
                 )
+            for k in range(2):
                 nc.vector.tensor_tensor(
-                    out=v[:], in0=pc, in1=w_pos[:, lo:hi].unsqueeze(1).to_broadcast(wide), op=ALU.add
+                    out=rows(k, 2), in0=rest[k][:].unsqueeze(2).to_broadcast(thrice), in1=rows(k, 1), op=ALU.subtract
                 )
-                nc.vector.tensor_scalar(out=u[:], in0=u[:], scalar1=1.0, scalar2=None, op0=ALU.add)
-                nc.vector.tensor_scalar(out=v[:], in0=v[:], scalar1=-0.5 / N, scalar2=None, op0=ALU.mult)
-            left = [u, v]
-            for lev in range(3):
-                got = []
-                for k in range(2):
-                    rows = uvt[k][:, :, 0 : 9 * H].rearrange("p j (a c h) -> p j a c h", a=3, c=3)
-                    dst = rows[:, :, lev, :, lo:hi] if k == 0 else rows[:, :, :, lev, lo:hi]
-                    nc.vector.tensor_copy(out=dst, in_=left[k][:].unsqueeze(2).to_broadcast([P, R, 3, n]))
-                    got.append(dst[:, :, 0, :])
-                if lev < 2:
-                    for k in range(2):
-                        rest = sb(f"rest{lo}{k}{lev}", wide, F32)
-                        nc.vector.tensor_tensor(out=rest[:], in0=left[k][:], in1=got[k], op=ALU.subtract)
-                        left[k] = rest
 
         def consts():
-            nc.vector.tensor_scalar(out=w_pos[:], in0=w_bf[:], scalar1=float(N), scalar2=None, op0=ALU.mult)
-            nc.vector.tensor_copy(out=bias[:], in_=b_bf[:])
-            nc.vector.tensor_scalar(out=w_inv[:], in0=w_pos[:], scalar1=0.0, scalar2=None, op0=ALU.is_equal)
-            nc.vector.tensor_tensor(out=w_inv[:], in0=w_inv[:], in1=w_pos[:], op=ALU.add)
+            nc.gpsimd.tensor_scalar(out=w_pos[:], in0=w_bf[:], scalar1=float(N), scalar2=0.0, op0=ALU.mult, op1=ALU.add)
+            nc.gpsimd.tensor_copy(out=bias[:], in_=b_bf[:])
+            nc.gpsimd.tensor_scalar(
+                out=w_inv[:], in0=w_pos[:], scalar1=0.0, scalar2=None, op0=ALU.is_equal
+            )
+            nc.gpsimd.tensor_tensor(out=w_inv[:], in0=w_inv[:], in1=w_pos[:], op=ALU.add)
+
+        def invert():
             nc.vector.reciprocal(w_inv[:], w_inv[:])
 
         gts = {}
+
+        def round_ident():
+            nc.vector.tensor_copy(out=ident16[:], in_=ident[:])
 
         def turn_gain():
             gts[0] = psum.tile([P, P], BF16, name="gt", tag="t", bufs=BUFS["t"])
@@ -366,37 +391,37 @@ def tile_esmcontactheadapc_w4_kernel(
         def copy_gain():
             nc.vector.tensor_copy(out=gain[:].rearrange("p h t -> p (h t)"), in_=gts[0][:, 0 : H * T])
 
-        zs = {}
+        z2 = {}
 
         def turn_rt():
-            zs["u"] = bank("rt", "l", dtype=BF16)
+            z2["u"] = bank("rt", "l", dtype=BF16)
             for j in range(R):
-                nc.tensor.transpose(zs["u"][:, j * P : (j + 1) * P], uvt[0][:, j, :], ident16[:])
+                nc.tensor.transpose(z2["u"][:, j * P : (j + 1) * P], uvt[0][:, j, :], ident16[:])
 
         def turn_vt():
-            zs["v"] = bank("vt", "l", dtype=BF16)
+            z2["v"] = bank("vt", "l", dtype=BF16)
             for j in range(R):
-                nc.tensor.transpose(zs["v"][:, j * P : (j + 1) * P], uvt[1][:, j, :], ident16[:])
+                nc.tensor.transpose(z2["v"][:, j * P : (j + 1) * P], uvt[1][:, j, :], ident16[:])
 
         def copy_rt():
-            nc.scalar.copy(out=ru[:], in_=zs["u"][:])
+            nc.scalar.copy(out=ru[:], in_=z2["u"][:])
 
         def copy_vt():
-            nc.vector.tensor_copy(out=rv[:], in_=zs["v"][:])
+            nc.vector.tensor_copy(out=rv[:], in_=z2["v"][:])
 
         def turn_acc(i):
-            zs[i] = bank(f"z{i}", ["p","p","p","l"][i])
+            z2[i] = bank(f"y{i}", "p")
             for j in range(R):
                 nc.tensor.matmul(
-                    zs[i][:, j * P : (j + 1) * P], lhsT=acc[j][:, i * P : (i + 1) * P], rhs=ident[:],
+                    z2[i][:, j * P : (j + 1) * P], lhsT=acc[j][:, i * P : (i + 1) * P], rhs=ident[:],
                     is_transpose=True, start=(j == 0), stop=False,
                 )
 
         def outer(i):
-            nc.tensor.matmul(zs[i][:], lhsT=ru[:, i * P : (i + 1) * P], rhs=rv[:], start=False, stop=True)
+            nc.tensor.matmul(z2[i][:], lhsT=ru[:, i * P : (i + 1) * P], rhs=rv[:], start=False, stop=True)
 
         def combine(i):
-            nc.vector.tensor_tensor(out=res[i][:], in0=zs[i][:], in1=acc[i][:], op=ALU.add)
+            nc.vector.tensor_tensor(out=res[i][:], in0=z2[i][:], in1=acc[i][:], op=ALU.add)
 
         def sigmoid(i):
             nc.scalar.activation(out=osb[i][:], in_=res[i][:], func=ACT.Sigmoid, bias=bias[:])
@@ -404,269 +429,282 @@ def tile_esmcontactheadapc_w4_kernel(
         def store(i):
             nc.sync.dma_start(out=out[i * P : (i + 1) * P, :], in_=osb[i][:])
 
+        widen_x(1)
+        round_ident()
         widen_x(0)
-        perm_w("k", 0)
+        widen_x(2)
+        perm_s("k", 1, H)
         turn_x(0)
         scale_x(0)
-        widen_x(2)
-        perm_s("k")
+        perm_w("k", 1)
+        quant_x(0)
+        perm_s("k", 0, 1)
+        perm_w("k", 0)
         widen_x(3)
+        turn_x(1)
+        proj("k", 1, 0)
+        proj("k", 0, 0)
         turn_x(2)
         turn_x(3)
-        quant_x(0)
-        proj("k", 1, 0)
-        scale_x(2)
-        widen_x(1)
-        turn_x(1)
-        quant_x(2)
-        scale_x(3)
         turn_gain()
-        perm_s("q")
-        copy_gain()
-        proj("k", 1, 2)
-        proj("k", 0, 2)
-        quant_x(3)
-        empty("k", 1, 0)
-        empty("k", 1, 2)
-        perm_w("q", 0)
-        empty("k", 0, 2)
-        proj("k", 0, 0)
-        empty("k", 0, 0)
         scale_x(1)
-        proj("k", 0, 3)
-        empty("k", 0, 3)
         quant_x(1)
-        proj("q", 0, 3)
-        proj("q", 0, 2)
-        proj("k", 0, 1)
-        empty("q", 0, 3)
-        empty("q", 0, 2)
-        perm_w("k", 1)
-        proj("q", 0, 1)
-        proj("k", 1, 3)
-        empty("k", 0, 1)
-        empty("q", 0, 1)
-        proj("k", 2, 0)
-        quant("k", 0, 0, N)
-        proj("q", 0, 0)
-        quant("q", 0, 256, N)
-        empty("k", 1, 3)
-        perm_w("q", 1)
-        score(0, 3)
-        empty("q", 0, 0)
-        proj("k", 2, 2)
-        empty("k", 2, 0)
-        score(0, 2)
-        empty("k", 2, 2)
-        proj("q", 2, 2)
-        row_max(0, 3)
+        empty("k", 0, 0)
         proj("k", 1, 1)
-        proj("k", 2, 1)
-        row_max(0, 2)
-        negate(0, 3)
-        quant("q", 0, 0, 256)
-        expo(0, 3)
-        negate(0, 2)
-        score(0, 0)
-        empty("q", 2, 2)
-        proj("q", 1, 2)
-        empty("k", 1, 1)
-        expo(0, 2)
-        empty("k", 2, 1)
-        recip(0, 3)
         consts()
-        row_max(0, 0)
-        proj("q", 1, 3)
-        recip(0, 2)
-        score(0, 1)
-        empty("q", 1, 2)
-        empty("q", 1, 3)
-        negate(0, 0)
-        expo(0, 0)
-        row_max(0, 1)
-        proj("k", 3, 3)
-        proj("k", 2, 3)
-        empty("k", 3, 3)
-        quant("q", 1, 256, N)
-        negate(0, 1)
-        proj("q", 1, 1)
-        recip(0, 0)
-        quant("k", 1, 0, N)
-        empty("k", 2, 3)
-        empty("q", 1, 1)
-        proj("q", 2, 3)
+        empty("k", 1, 0)
+        perm_w("q", 0)
+        scale_x(2)
+        proj("k", 0, 1)
+        empty("k", 1, 1)
+        quant_x(2)
+        perm_s("q", 0, H)
+        proj("k", 0, 2)
+        scale_x(3)
+        copy_gain()
+        empty("k", 0, 1)
+        proj("q", 0, 0)
+        empty("k", 0, 2)
+        proj("q", 0, 2)
+        proj("k", 1, 2)
+        quant_x(3)
+        empty("q", 0, 0)
+        empty("k", 1, 2)
+        proj("q", 0, 1)
+        proj("k", 0, 3)
+        perm_w("k", 2)
+        empty("q", 0, 2)
+        proj("k", 1, 3)
+        empty("q", 0, 1)
+        proj("k", 2, 1)
+        empty("k", 0, 3)
+        perm_w("q", 1)
+        empty("k", 1, 3)
+        perm_w("q", 3)
+        proj("q", 0, 3)
+        quant("q", 0, 256, 384)
+        quant("q", 0, 128, 256)
+        quant("k", 0, 0, N)
+        quant("q", 0, 0, 128)
         proj("q", 1, 0)
-        expo(0, 1)
-        score(1, 3)
-        weigh(0, 2)
-        empty("q", 2, 3)
-        recip(0, 1)
-        weigh(0, 3)
-        proj("k", 3, 2)
-        empty("k", 3, 2)
+        perm_w("q", 2)
+        score(0, 1)
+        score(0, 2)
+        empty("k", 2, 1)
+        empty("q", 0, 3)
+        row_max(0, 1)
+        row_max(0, 2)
         empty("q", 1, 0)
-        weigh(0, 0)
-        row_max(1, 3)
-        quant("q", 1, 0, 256)
-        score(1, 2)
-        row_max(1, 2)
-        weigh(0, 1)
-        negate(1, 3)
-        quant("q", 2, 256, N)
-        expo(1, 3)
-        proj("k", 3, 1)
-        turn_p(0, 0)
-        negate(1, 2)
-        colsum(0, 0)
-        recip(1, 3)
-        expo(1, 2)
-        quant("k", 2, 0, N)
-        score(1, 0)
-        row_max(1, 0)
-        proj("q", 2, 0)
-        negate(1, 0)
+        negate(0, 1)
         proj("q", 2, 1)
-        recip(1, 2)
-        empty("k", 3, 1)
-        score(2, 3)
-        weigh(1, 3)
-        score(1, 1)
-        turn_p(0, 1)
-        expo(1, 0)
-        proj("q", 3, 2)
-        score(2, 2)
-        empty("q", 2, 0)
-        row_max(2, 3)
-        proj("q", 3, 3)
-        row_max(1, 1)
-        negate(2, 3)
-        expo(2, 3)
+        proj("q", 2, 0)
         empty("q", 2, 1)
-        weigh(1, 2)
-        proj("k", 3, 0)
+        negate(0, 2)
+        empty("q", 2, 0)
+        score(0, 0)
+        proj("q", 1, 1)
+        quant("q", 0, 384, 512)
+        proj("q", 2, 2)
+        expo(0, 1)
+        row_max(0, 0)
+        perm_w("k", 3)
+        proj("q", 2, 3)
+        empty("q", 1, 1)
+        negate(0, 0)
+        empty("q", 2, 2)
+        quant("k", 1, 0, N)
+        empty("q", 2, 3)
+        score(0, 3)
+        quant("q", 1, 0, 256)
+        expo(0, 2)
+        row_max(0, 3)
+        proj("q", 1, 2)
+        proj("k", 2, 0)
+        expo(0, 0)
+        empty("k", 2, 0)
+        empty("q", 1, 2)
+        proj("q", 1, 3)
+        score(1, 1)
+        recip(0, 1)
+        score(1, 0)
+        empty("q", 1, 3)
+        negate(0, 3)
+        proj("k", 2, 2)
+        expo(0, 3)
+        row_max(1, 1)
+        proj("q", 3, 2)
+        quant("q", 1, 256, N)
+        empty("k", 2, 2)
+        recip(0, 3)
+        recip(0, 0)
+        proj("k", 2, 3)
+        row_max(1, 0)
         negate(1, 1)
-        recip(1, 0)
-        turn_p(0, 3)
-        recip(2, 3)
+        score(1, 3)
         expo(1, 1)
+        weave(2, 0, 256)
+        recip(0, 2)
         empty("q", 3, 2)
+        proj("k", 3, 2)
+        weave(2, 256, N)
+        negate(1, 0)
+        proj("k", 3, 1)
+        empty("k", 2, 3)
+        weigh(0, 1)
+        row_max(1, 3)
+        quant("k", 2, 0, N)
+        expo(1, 0)
+        quant("q", 3, 256, 384)
+        proj("k", 3, 0)
+        negate(1, 3)
+        empty("k", 3, 2)
+        recip(1, 0)
+        score(1, 2)
         quant("q", 2, 0, 256)
-        colsum(0, 1)
-        gather(1, 3)
-        recip(1, 1)
-        gather(1, 2)
-        weigh(2, 3)
-        empty("k", 3, 0)
-        weigh(1, 1)
-        row_max(2, 2)
-        score(2, 0)
-        negate(2, 2)
-        weigh(1, 0)
-        empty("q", 3, 3)
-        expo(2, 2)
-        colsum(0, 3)
-        row_max(2, 0)
-        negate(2, 0)
-        score(2, 1)
-        quant("q", 3, 256, N)
         proj("q", 3, 0)
-        turn_p(1, 1)
-        quant("k", 3, 0, N)
-        expo(2, 0)
-        gather(2, 3)
-        colsum(1, 1)
-        turn_p(1, 3)
-        row_max(2, 1)
-        recip(2, 0)
-        score(3, 3)
-        recip(2, 2)
-        row_max(3, 3)
-        score(3, 2)
-        negate(2, 1)
+        weigh(0, 3)
+        row_max(1, 2)
+        score(2, 0)
+        expo(1, 3)
+        quant("q", 2, 256, N)
+        empty("k", 3, 1)
+        weigh(0, 0)
+        negate(1, 2)
+        recip(1, 1)
+        row_max(2, 0)
+        expo(1, 2)
         proj("q", 3, 1)
-        weigh(2, 2)
-        empty("q", 3, 0)
+        empty("k", 3, 0)
+        score(2, 2)
         empty("q", 3, 1)
-        expo(2, 1)
-        gather(1, 0)
-        turn_p(0, 2)
-        recip(2, 1)
-        colsum(1, 3)
-        turn_p(1, 0)
-        quant("q", 3, 0, 256)
-        gather(1, 1)
-        negate(3, 3)
-        colsum(0, 2)
+        weigh(0, 2)
+        row_max(2, 2)
+        recip(1, 2)
+        proj("k", 3, 3)
+        negate(2, 0)
+        score(2, 3)
+        row_max(2, 3)
+        turn_col(0, 0)
+        weigh(1, 0)
+        empty("k", 3, 3)
+        empty("q", 3, 0)
+        weigh(1, 1)
+        turn_col(0, 1)
+        negate(2, 2)
+        expo(2, 0)
+        turn_col(0, 2)
+        quant("k", 3, 0, N)
+        turn_col(0, 3)
+        negate(2, 3)
+        quant("q", 3, 0, 128)
+        score(2, 1)
+        quant("q", 3, 128, 256)
+        recip(1, 3)
+        expo(2, 2)
+        proj("q", 3, 3)
+        expo(2, 3)
+        colsum(0)
+        weigh(1, 3)
+        score(3, 2)
+        row_max(2, 1)
+        recip(2, 2)
         row_max(3, 2)
-        expo(3, 3)
         score(3, 0)
-        row_max(3, 0)
-        weigh(2, 1)
-        weigh(2, 0)
-        recip(3, 3)
-        score(3, 1)
-        row_max(3, 1)
-        turn_p(2, 2)
-        colsum(1, 0)
-        negate(3, 0)
-        expo(3, 0)
-        negate(3, 2)
-        negate(3, 1)
-        weigh(3, 3)
-        turn_p(2, 1)
-        expo(3, 1)
-        recip(3, 0)
-        weigh(3, 0)
-        turn_last(3)
-        colsum(2, 2)
-        turn_last(0)
-        turn_p(2, 3)
-        recip(3, 1)
-        turn_p(2, 0)
-        expo(3, 2)
-        colsum_last(3)
-        colsum(2, 1)
-        recip(3, 2)
-        weigh(3, 1)
-        turn_p(1, 2)
-        weigh(3, 2)
-        colsum_last(0)
-        colsum(1, 2)
-        turn_last(2)
-        colsum_last(2)
-        gather(3, 3)
-        turn_last(1)
-        colsum(2, 0)
-        colsum_last(1)
-        colsum(2, 3)
-        split(0, 4)
-        turn_rt()
-        gather(2, 1)
-        gather(2, 2)
-        copy_rt()
+        weigh(1, 2)
+        negate(2, 1)
+        expo(2, 1)
+        weigh(2, 2)
         gather(2, 0)
-        gather(3, 2)
-        turn_vt()
-        gather(3, 1)
+        gather(1, 0)
+        negate(3, 2)
+        empty("q", 3, 3)
+        row_max(3, 0)
+        turn_col(1, 0)
+        quant("q", 3, 384, 512)
+        invert()
+        recip(2, 0)
+        weigh(2, 0)
+        recip(2, 3)
+        turn_col(1, 1)
+        expo(3, 2)
+        turn_col(1, 2)
+        turn_col(1, 3)
+        score(3, 1)
+        negate(3, 0)
+        recip(2, 1)
+        colsum(1)
+        row_max(3, 1)
+        score(3, 3)
+        row_max(3, 3)
         gather(3, 0)
+        gather(2, 1)
+        expo(3, 0)
+        negate(3, 1)
+        turn_col(2, 0)
+        recip(3, 0)
+        weigh(2, 1)
+        negate(3, 3)
+        recip(3, 2)
+        uv(1)
+        weigh(2, 3)
+        gather(0, 0)
+        turn_col(2, 1)
+        uv(0)
+        expo(3, 1)
+        turn_col(2, 2)
+        turn_col(2, 3)
+        gather(1, 1)
+        expo(3, 3)
+        weigh(3, 0)
+        recip(3, 1)
+        gather(0, 1)
+        weigh(3, 1)
+        gather(1, 2)
+        colsum(2)
+        recip(3, 3)
+        gather(0, 2)
+        weigh(3, 2)
+        uv(2)
+        weigh(3, 3)
+        turn_col(3, 0)
+        turn_col(3, 1)
+        turn_col(3, 2)
+        turn_col(3, 3)
+        gather(3, 1)
+        gather(2, 2)
+        gather(3, 2)
+        gather_last(0)
+        colsum(3)
+        gather_last(3)
+        gather_last(2)
+        gather_last(1)
+        keep_z(3)
+        uv(3)
+        split()
+        keep_z(0)
+        turn_vt()
+        keep_z(2)
+        turn_rt()
+        keep_z(1)
+        copy_rt()
         turn_acc(2)
-        turn_acc(3)
-        turn_acc(0)
         copy_vt()
+        turn_acc(3)
         outer(2)
-        combine(2)
-        sigmoid(2)
-        outer(0)
-        store(2)
-        turn_acc(1)
-        combine(0)
         outer(3)
+        turn_acc(1)
+        combine(2)
         combine(3)
+        sigmoid(2)
         outer(1)
-        sigmoid(0)
-        sigmoid(3)
-        store(0)
         combine(1)
-        sigmoid(1)
+        turn_acc(0)
+        outer(0)
+        sigmoid(3)
+        store(2)
         store(3)
+        combine(0)
+        sigmoid(1)
+        sigmoid(0)
         store(1)
+        store(0)

from contextlib import ExitStack

import concourse.mybir as mybir
from concourse.masks import make_identity

N, D, H, E = 512, 1024, 4, 512
FLOPS = 2 * (2 * N * D * H * E) + H * 2 * N * N * E

F32 = mybir.dt.float32
BF16 = mybir.dt.bfloat16
I32 = mybir.dt.int32
U32 = mybir.dt.uint32
U8 = mybir.dt.uint8
FP8 = mybir.dt.float8_e4m3fn
FP8X4 = mybir.dt.float8_e4m3fn_x4
FP4X4 = mybir.dt.float4_e2m1fn_x4
ALU = mybir.AluOpType
ACT = mybir.ActivationFunctionType
AX = mybir.AxisListType

P = 128
T = 4
G = D // 512
R = N // P
S = H * R
SCALE = 1.0 / E**0.5


def tile_esmcontactheadapc_w4_kernel(
    tc, x_bytes, x_scale, w_q_words, w_q_scales, g_q, w_k_words, w_k_scales, w_head, b_head, out
):
    nc = tc.nc
    with ExitStack() as ctx:
        keep = ctx.enter_context(tc.tile_pool(name="keep", bufs=1))
        psum = ctx.enter_context(tc.psum_pool(name="psum", bufs=1))
        ctx.enter_context(tc.manual_schedule())

        def sb(name, shape, dtype, align=64):
            return keep.tile(shape, dtype, name=name, align_bytes=align)

        BUFS = {"p": 4, "l": 3, "t": 1}

        def bank(name, tag, shape=(P, 512), dtype=F32):
            return psum.tile(list(shape), dtype, name=name, tag=tag, bufs=BUFS[tag])

        xb = [sb(f"xb{i}", [P, D], U8) for i in range(R)]
        xscale = sb("xscale", [P, G, T], F32)
        xs = [sb(f"xs{i}", [P, D], BF16) for i in range(R)]
        xg = [sb(f"xg{i}", [P, G, P, T], BF16) for i in range(R)]
        xc = sb("xc", [P, G, N], U32)
        xcs = sb("xcs", [P, G, N], U8)
        words = {"q": w_q_words, "k": w_k_words}
        scales = {"q": w_q_scales, "k": w_k_scales}
        wraw = {(s, h): sb(f"wraw_{s}{h}", [P, G, 2 * E], U8) for s in "qk" for h in range(H)}
        wp = {(s, h): sb(f"wp_{s}{h}", [P, T, G, 2 * P], U8) for s in "qk" for h in range(H)}
        sraw = {s: sb(f"sraw_{s}", [P, G, H * E], U8) for s in "qk"}
        sp = {s: sb(f"sp_{s}", [P, T, G, H * P], U8) for s in "qk"}
        grp = {(s, h): sb(f"grp_{s}{h}", [P, N, T], BF16) for s in "qk" for h in range(H)}
        code = {(s, h): sb(f"code_{s}{h}", [P, N], U32) for s in "qk" for h in range(H)}
        cscl = {(s, h): sb(f"cscl_{s}{h}", [P, N], U8) for s in "qk" for h in range(H)}
        flat = {h: sb(f"flat{h}", [P, T, N], BF16) for h in [2]}
        e = {(h, i): sb(f"e{h}{i}", [P, N], F32) for h in range(H) for i in range(R)}
        p = {(h, i): sb(f"p{h}{i}", [P, N], F32) for h in range(H) for i in range(R)}
        acc = [sb(f"acc{i}", [P, N], F32) for i in range(R)]
        junk = [sb(f"junk{i}", [P, N], BF16) for i in range(2)]
        ident = sb("ident", [P, P], F32)
        ident16 = sb("ident16", [P, P], BF16)
        g_rows = sb("g_rows", [P, P], BF16)
        gain = sb("gain", [P, H, T], F32)
        w_bf = sb("w_bf", [P, H], BF16)
        b_bf = sb("b_bf", [P, 1], BF16)
        w_pos = sb("w_pos", [P, H], F32)
        w_inv = sb("w_inv", [P, H], F32)
        bias = sb("bias", [P, 1], F32)
        zero = sb("zero", [P, 1], F32)
        dummy = sb("dummy", [P, 1], F32)
        rowmax = sb("rowmax", [P, S], F32)
        nbias = sb("nbias", [P, S], F32)
        rowsum = sb("rowsum", [P, S], F32)
        cfac = sb("cfac", [P, S], F32)
        rinv = sb("rinv", [P, S], F32)
        pcol = sb("pcol", [P, S], F32)
        rest = [sb(f"rest{k}", [P, R, H], F32) for k in range(2)]
        u_all = sb("u_all", [P, R, H], F32)
        v_all = sb("v_all", [P, R, H], F32)
        uvt = [sb(f"uvt{k}", [P, R, P], BF16) for k in range(2)]
        ru = sb("ru", [P, N], BF16)
        rv = sb("rv", [P, N], BF16)
        res = [sb(f"res{i}", [P, N], F32) for i in range(R)]
        osb = [sb(f"osb{i}", [P, N], F32) for i in range(R)]

        def load_x(i):
            nc.sync.dma_start(out=xb[i][:], in_=x_bytes[i * P : (i + 1) * P, :])

        def load_w(s, h):
            nc.sync.dma_start(
                out=wraw[s, h][:], in_=words[s][:, :, 2 * E * h : 2 * E * (h + 1)].rearrange("g p c -> p g c")
            )

        def load_s(s):
            for q in range(4):
                nc.sync.dma_start(
                    out=sraw[s][32 * q : 32 * q + 4].bitcast(I32),
                    in_=scales[s].bitcast(I32)[:, 4 * q : 4 * q + 4, :].rearrange("g q n -> q g n"),
                )

        idle = sb("idle", [P, N], BF16)
        nc.vector.memset(idle[:], 0.0)
        wb = bank("warm", "l")
        for k in range(4):
            nc.tensor.matmul(wb[:], lhsT=idle[:, 0:P], rhs=idle[:], start=True, stop=True)
        nc.vector.memset(sraw["k"][:].rearrange("p g c -> p (g c)").bitcast(I32), 0)
        nc.vector.memset(zero[:], 0.0)
        nc.vector.memset(sraw["q"][:].rearrange("p g c -> p (g c)").bitcast(I32), 0)
        make_identity(nc, ident[:])
        nc.gpsimd.memset(g_rows[:], 0.0)
        nc.gpsimd.memset(uvt[0][:], 0.0)
        nc.gpsimd.memset(uvt[1][:], 0.0)

        nc.scalar.dma_start(out=xscale[:], in_=x_scale.rearrange("o (g p t) -> p (o g) t", g=G, t=T))
        nc.scalar.activation(out=dummy[:], in_=zero[:], func=ACT.Exp)
        load_x(0)
        load_s("k")
        load_w("k", 0)
        load_x(1)
        load_w("k", 1)
        load_x(2)
        load_x(3)
        load_s("q")
        load_w("q", 0)
        load_w("q", 1)
        load_w("k", 2)
        load_w("q", 2)
        load_w("k", 3)
        load_w("q", 3)
        for h in range(H):
            nc.scalar.dma_start(
                out=g_rows[T * h : T * (h + 1), :].rearrange("t (b i) -> t b i", i=8),
                in_=g_q[E * h : E * (h + 1)].rearrange("(b t i) -> t b i", t=T, i=8),
            )
        nc.scalar.dma_start(out=w_bf[:], in_=w_head.partition_broadcast(P))
        nc.scalar.dma_start(out=b_bf[:], in_=b_head.partition_broadcast(P))

        def widen_x(i):
            if i in [0]:
                nc.vector.tensor_copy(out=xs[i][:], in_=xb[i][:].bitcast(FP8))
            else:
                nc.scalar.copy(out=xs[i][:], in_=xb[i][:].bitcast(FP8))

        xts = {}

        def turn_x(i):
            w = xs[i][:].bitcast(F32)
            xts[i] = bank(f"xt{i}", "l", (P, G, 2, P))
            for g in range(G):
                for u in range(2):
                    nc.tensor.transpose(xts[i][:, g, u, :], w[:, 256 * g + u : 256 * (g + 1) : 2], ident[:])

        def scale_x(i):
            for g in range(G):
                nc.vector.tensor_tensor(
                    out=xg[i][:, g].rearrange("p r (u e) -> p r u e", u=2),
                    in0=xts[i][:, g].bitcast(BF16).rearrange("p u (r e) -> p r u e", e=2),
                    in1=xscale[:, g : g + 1, :].to_broadcast([P, P, T]).rearrange("p r (u e) -> p r u e", u=2),
                    op=ALU.mult,
                )

        def quant_x(i):
            for g in range(G):
                r = slice(i * P, (i + 1) * P)
                nc.vector.quantize_mx(
                    out=xc[:, g, r].bitcast(FP8X4), scales=xcs[:, g, r], in_=xg[i][:, g].rearrange("p r t -> p (r t)")
                )

        def perm_w(s, h):
            nc.vector.tensor_copy(
                out=wp[s, h][:].rearrange("p t g c -> p t (g c)").bitcast(I32).rearrange("p t (b i) -> p t b i", i=4),
                in_=wraw[s, h][:].rearrange("p g c -> p (g c)").bitcast(I32).rearrange("p (b t i) -> p t b i", t=T, i=4),
            )

        def perm_s(s, lo, hi):
            for g in range(G):
                nc.vector.tensor_copy(
                    out=sp[s][:, :, g, P * lo : P * hi].bitcast(I32).rearrange("p t (b i) -> p t b i", i=2),
                    in_=sraw[s][:, g, E * lo : E * hi].bitcast(I32).rearrange("p (b t i) -> p t b i", t=T, i=2),
                )

        def mx(dst, s, h, t, lo, hi):
            for g in range(G):
                nc.tensor.matmul_mx(
                    out=dst,
                    lhsT=wp[s, h][:, t, g, :].bitcast(FP4X4),
                    lhsT_scale=sp[s][:, t, g, h * P : (h + 1) * P],
                    rhs=xc[:, g, lo:hi].bitcast(FP8X4),
                    rhs_scale=xcs[:, g, lo:hi],
                    start=(g == 0),
                    stop=(g == G - 1),
                )

        pss = {}

        def proj(s, h, i):
            if s == "q" and h in flat:
                pss[s, h, i] = bank(f"pq_{h}{i}", "p")
                mx(pss[s, h, i][:], s, h, i, 0, N)
                return
            pss[s, h, i] = bank(f"ps_{s}{h}{i}", "p", (P, T, P))
            for t in range(T):
                mx(pss[s, h, i][:, t, :], s, h, t, i * P, (i + 1) * P)

        def empty(s, h, i):
            ps = pss[s, h, i]
            if s == "q" and h in flat:
                nc.scalar.activation(out=flat[h][:, i, :], in_=ps[:], func=ACT.Copy, scale=gain[:, h, i : i + 1])
                return
            dst = grp[s, h][:, i * P : (i + 1) * P, :]
            src = ps[:].rearrange("p t n -> p n t")
            if s == "k":
                nc.scalar.copy(out=dst, in_=src)
            else:
                nc.vector.tensor_tensor(
                    out=dst, in0=src, in1=gain[:, h : h + 1, :].to_broadcast([P, P, T]), op=ALU.mult
                )

        def weave(h, lo, hi):
            if h in flat:
                src = flat[h][:, :, lo:hi].rearrange("p t n -> p n t")
                nc.gpsimd.tensor_scalar(
                    out=grp["q", h][:, lo:hi, :], in0=src, scalar1=1.0, scalar2=0.0, op0=ALU.mult, op1=ALU.add
                )

        def quant(s, h, lo, hi):
            nc.vector.quantize_mx(
                out=code[s, h][:, lo:hi].bitcast(FP8X4),
                scales=cscl[s, h][:, lo:hi],
                in_=grp[s, h][:, lo:hi, :].rearrange("p n t -> p (n t)"),
            )

        logits = {}

        def score(h, i):
            lg = bank(f"lg{h}{i}", "l")
            r = slice(i * P, (i + 1) * P)
            nc.tensor.matmul_mx(
                out=lg[:],
                lhsT=code["q", h][:, r].bitcast(FP8X4),
                lhsT_scale=cscl["q", h][:, r],
                rhs=code["k", h][:].bitcast(FP8X4),
                rhs_scale=cscl["k", h][:],
                start=True,
                stop=True,
            )
            logits[h, i] = lg

        def row_max(h, i):
            c = h * R + i
            nc.vector.tensor_reduce(out=rowmax[:, c : c + 1], in_=logits[h, i][:], axis=AX.X, op=ALU.max)

        def negate(h, i):
            c = h * R + i
            nc.scalar.activation(out=nbias[:, c : c + 1], in_=rowmax[:, c : c + 1], func=ACT.Copy, scale=-SCALE)

        def expo(h, i):
            c = h * R + i
            nc.scalar.activation(
                out=e[h, i][:], in_=logits[h, i][:], func=ACT.Exp, bias=nbias[:, c : c + 1], scale=SCALE,
                accum_out=rowsum[:, c : c + 1],
            )

        def recip(h, i):
            c = h * R + i
            nc.vector.reciprocal(rinv[:, c : c + 1], rowsum[:, c : c + 1])

        def weigh(h, i):
            c = h * R + i
            if (h, i) in []:
                nc.vector.tensor_tensor(
                    out=cfac[:, c : c + 1], in0=rinv[:, c : c + 1], in1=w_pos[:, h : h + 1], op=ALU.mult
                )
                nc.scalar.activation(out=p[h, i][:], in_=e[h, i][:], func=ACT.Copy, scale=cfac[:, c : c + 1])
                return
            on_vector = (h, i) in [(3, 0),(3, 1),(3, 2),(3, 3)]
            eng = nc.vector if on_vector else nc.gpsimd
            n = 1 if on_vector else 1
            for k in range(n):
                cols = slice(k * N // n, (k + 1) * N // n)
                eng.tensor_scalar(
                    out=p[h, i][:, cols], in0=e[h, i][:, cols], scalar1=rinv[:, c : c + 1],
                    scalar2=w_pos[:, h : h + 1], op0=ALU.mult, op1=ALU.mult,
                )

        zs = {}
        writes = [0] * R

        def add_turned(j, h, i):
            if j not in zs:
                zs[j] = bank(f"z{j}", "p")
            nc.tensor.matmul(
                zs[j][:, i * P : (i + 1) * P], lhsT=p[h, i][:, j * P : (j + 1) * P], rhs=ident[:],
                is_transpose=True, start=(writes[j] == 0), stop=(writes[j] == S - 1),
            )
            writes[j] += 1

        def gather(j, h):
            for i in range(R):
                add_turned(j, h, i)

        def gather_last(i):
            for j in range(R):
                add_turned(j, H - 1, i)

        def keep_z(j):
            if j in [0,1]:
                nc.vector.tensor_copy(out=acc[j][:], in_=zs[j][:])
            else:
                nc.scalar.copy(out=acc[j][:], in_=zs[j][:])

        tps = {}

        turned = [0] * H

        def turn_col(h, i):
            if h not in tps:
                tps[h] = bank(f"tp{h}", "t", (P, R, P))
            for j in range(R):
                nc.tensor.matmul(
                    tps[h][:, j, :], lhsT=p[h, i][:, j * P : (j + 1) * P], rhs=ident[:], is_transpose=True,
                    start=(turned[h] == 0), stop=(turned[h] == S - 1),
                )
                turned[h] += 1

        def colsum(h):
            if h in [0,1,2]:
                for j in range(R):
                    nc.scalar.activation(
                        out=junk[h % 2][:, j * P : (j + 1) * P], in_=tps[h][:, j, :], func=ACT.Copy,
                        accum_out=pcol[:, h * R + j : h * R + j + 1],
                    )
            else:
                nc.vector.tensor_reduce(out=pcol[:, h * R : (h + 1) * R], in_=tps[h][:], axis=AX.X, op=ALU.add)

        def uv(h):
            pc = pcol[:, h * R : (h + 1) * R]
            nc.vector.tensor_scalar(
                out=u_all[:, :, h], in0=pc, scalar1=w_inv[:, h : h + 1], scalar2=1.0, op0=ALU.mult, op1=ALU.add
            )
            nc.vector.tensor_scalar(
                out=v_all[:, :, h], in0=pc, scalar1=w_pos[:, h : h + 1], scalar2=-0.5 / N, op0=ALU.add, op1=ALU.mult
            )

        def rows(k, lev):
            cells = uvt[k][:, :, 0 : 9 * H].rearrange("p j (a c h) -> p j a c h", a=3, c=3)
            return cells[:, :, lev, :, :] if k == 0 else cells[:, :, :, lev, :]

        def split():
            thrice = [P, R, 3, H]
            whole = [u_all, v_all]
            for k in range(2):
                nc.vector.tensor_copy(out=rows(k, 0), in_=whole[k][:].unsqueeze(2).to_broadcast(thrice))
            for k in range(2):
                nc.vector.tensor_tensor(out=rest[k][:], in0=whole[k][:], in1=rows(k, 0)[:, :, 0, :], op=ALU.subtract)
            for k in range(2):
                nc.vector.tensor_tensor(
                    out=rows(k, 1), in0=whole[k][:].unsqueeze(2).to_broadcast(thrice), in1=rows(k, 0), op=ALU.subtract
                )
            for k in range(2):
                nc.vector.tensor_tensor(
                    out=rows(k, 2), in0=rest[k][:].unsqueeze(2).to_broadcast(thrice), in1=rows(k, 1), op=ALU.subtract
                )

        def consts():
            nc.gpsimd.tensor_scalar(out=w_pos[:], in0=w_bf[:], scalar1=float(N), scalar2=0.0, op0=ALU.mult, op1=ALU.add)
            nc.gpsimd.tensor_copy(out=bias[:], in_=b_bf[:])
            nc.gpsimd.tensor_scalar(
                out=w_inv[:], in0=w_pos[:], scalar1=0.0, scalar2=None, op0=ALU.is_equal
            )
            nc.gpsimd.tensor_tensor(out=w_inv[:], in0=w_inv[:], in1=w_pos[:], op=ALU.add)

        def invert():
            nc.vector.reciprocal(w_inv[:], w_inv[:])

        gts = {}

        def round_ident():
            nc.vector.tensor_copy(out=ident16[:], in_=ident[:])

        def turn_gain():
            gts[0] = psum.tile([P, P], BF16, name="gt", tag="t", bufs=BUFS["t"])
            nc.tensor.transpose(gts[0][:], g_rows[:], ident16[:])

        def copy_gain():
            nc.vector.tensor_copy(out=gain[:].rearrange("p h t -> p (h t)"), in_=gts[0][:, 0 : H * T])

        z2 = {}

        def turn_rt():
            z2["u"] = bank("rt", "l", dtype=BF16)
            for j in range(R):
                nc.tensor.transpose(z2["u"][:, j * P : (j + 1) * P], uvt[0][:, j, :], ident16[:])

        def turn_vt():
            z2["v"] = bank("vt", "l", dtype=BF16)
            for j in range(R):
                nc.tensor.transpose(z2["v"][:, j * P : (j + 1) * P], uvt[1][:, j, :], ident16[:])

        def copy_rt():
            nc.scalar.copy(out=ru[:], in_=z2["u"][:])

        def copy_vt():
            nc.vector.tensor_copy(out=rv[:], in_=z2["v"][:])

        def turn_acc(i):
            z2[i] = bank(f"y{i}", "p")
            for j in range(R):
                nc.tensor.matmul(
                    z2[i][:, j * P : (j + 1) * P], lhsT=acc[j][:, i * P : (i + 1) * P], rhs=ident[:],
                    is_transpose=True, start=(j == 0), stop=False,
                )

        def outer(i):
            nc.tensor.matmul(z2[i][:], lhsT=ru[:, i * P : (i + 1) * P], rhs=rv[:], start=False, stop=True)

        def combine(i):
            nc.vector.tensor_tensor(out=res[i][:], in0=z2[i][:], in1=acc[i][:], op=ALU.add)

        def sigmoid(i):
            nc.scalar.activation(out=osb[i][:], in_=res[i][:], func=ACT.Sigmoid, bias=bias[:])

        def store(i):
            nc.sync.dma_start(out=out[i * P : (i + 1) * P, :], in_=osb[i][:])

        widen_x(1)
        round_ident()
        widen_x(0)
        widen_x(2)
        perm_s("k", 1, H)
        turn_x(0)
        scale_x(0)
        perm_w("k", 1)
        quant_x(0)
        perm_s("k", 0, 1)
        perm_w("k", 0)
        widen_x(3)
        turn_x(1)
        proj("k", 1, 0)
        proj("k", 0, 0)
        turn_x(2)
        turn_x(3)
        turn_gain()
        scale_x(1)
        quant_x(1)
        empty("k", 0, 0)
        proj("k", 1, 1)
        consts()
        empty("k", 1, 0)
        perm_w("q", 0)
        scale_x(2)
        proj("k", 0, 1)
        empty("k", 1, 1)
        quant_x(2)
        perm_s("q", 0, H)
        proj("k", 0, 2)
        scale_x(3)
        copy_gain()
        empty("k", 0, 1)
        proj("q", 0, 0)
        empty("k", 0, 2)
        proj("q", 0, 2)
        proj("k", 1, 2)
        quant_x(3)
        empty("q", 0, 0)
        empty("k", 1, 2)
        proj("q", 0, 1)
        proj("k", 0, 3)
        perm_w("k", 2)
        empty("q", 0, 2)
        proj("k", 1, 3)
        empty("q", 0, 1)
        proj("k", 2, 1)
        empty("k", 0, 3)
        perm_w("q", 1)
        empty("k", 1, 3)
        perm_w("q", 3)
        proj("q", 0, 3)
        quant("q", 0, 256, 384)
        quant("q", 0, 128, 256)
        quant("k", 0, 0, N)
        quant("q", 0, 0, 128)
        proj("q", 1, 0)
        perm_w("q", 2)
        score(0, 1)
        score(0, 2)
        empty("k", 2, 1)
        empty("q", 0, 3)
        row_max(0, 1)
        row_max(0, 2)
        empty("q", 1, 0)
        negate(0, 1)
        proj("q", 2, 1)
        proj("q", 2, 0)
        empty("q", 2, 1)
        negate(0, 2)
        empty("q", 2, 0)
        score(0, 0)
        proj("q", 1, 1)
        quant("q", 0, 384, 512)
        proj("q", 2, 2)
        expo(0, 1)
        row_max(0, 0)
        perm_w("k", 3)
        proj("q", 2, 3)
        empty("q", 1, 1)
        negate(0, 0)
        empty("q", 2, 2)
        quant("k", 1, 0, N)
        empty("q", 2, 3)
        score(0, 3)
        quant("q", 1, 0, 256)
        expo(0, 2)
        row_max(0, 3)
        proj("q", 1, 2)
        proj("k", 2, 0)
        expo(0, 0)
        empty("k", 2, 0)
        empty("q", 1, 2)
        proj("q", 1, 3)
        score(1, 1)
        recip(0, 1)
        score(1, 0)
        empty("q", 1, 3)
        negate(0, 3)
        proj("k", 2, 2)
        expo(0, 3)
        row_max(1, 1)
        proj("q", 3, 2)
        quant("q", 1, 256, N)
        empty("k", 2, 2)
        recip(0, 3)
        recip(0, 0)
        proj("k", 2, 3)
        row_max(1, 0)
        negate(1, 1)
        score(1, 3)
        expo(1, 1)
        weave(2, 0, 256)
        recip(0, 2)
        empty("q", 3, 2)
        proj("k", 3, 2)
        weave(2, 256, N)
        negate(1, 0)
        proj("k", 3, 1)
        empty("k", 2, 3)
        weigh(0, 1)
        row_max(1, 3)
        quant("k", 2, 0, N)
        expo(1, 0)
        quant("q", 3, 256, 384)
        proj("k", 3, 0)
        negate(1, 3)
        empty("k", 3, 2)
        recip(1, 0)
        score(1, 2)
        quant("q", 2, 0, 256)
        proj("q", 3, 0)
        weigh(0, 3)
        row_max(1, 2)
        score(2, 0)
        expo(1, 3)
        quant("q", 2, 256, N)
        empty("k", 3, 1)
        weigh(0, 0)
        negate(1, 2)
        recip(1, 1)
        row_max(2, 0)
        expo(1, 2)
        proj("q", 3, 1)
        empty("k", 3, 0)
        score(2, 2)
        empty("q", 3, 1)
        weigh(0, 2)
        row_max(2, 2)
        recip(1, 2)
        proj("k", 3, 3)
        negate(2, 0)
        score(2, 3)
        row_max(2, 3)
        turn_col(0, 0)
        weigh(1, 0)
        empty("k", 3, 3)
        empty("q", 3, 0)
        weigh(1, 1)
        turn_col(0, 1)
        negate(2, 2)
        expo(2, 0)
        turn_col(0, 2)
        quant("k", 3, 0, N)
        turn_col(0, 3)
        negate(2, 3)
        quant("q", 3, 0, 128)
        score(2, 1)
        quant("q", 3, 128, 256)
        recip(1, 3)
        expo(2, 2)
        proj("q", 3, 3)
        expo(2, 3)
        colsum(0)
        weigh(1, 3)
        score(3, 2)
        row_max(2, 1)
        recip(2, 2)
        row_max(3, 2)
        score(3, 0)
        weigh(1, 2)
        negate(2, 1)
        expo(2, 1)
        weigh(2, 2)
        gather(2, 0)
        gather(1, 0)
        negate(3, 2)
        empty("q", 3, 3)
        row_max(3, 0)
        turn_col(1, 0)
        quant("q", 3, 384, 512)
        invert()
        recip(2, 0)
        weigh(2, 0)
        recip(2, 3)
        turn_col(1, 1)
        expo(3, 2)
        turn_col(1, 2)
        turn_col(1, 3)
        score(3, 1)
        negate(3, 0)
        recip(2, 1)
        colsum(1)
        row_max(3, 1)
        score(3, 3)
        row_max(3, 3)
        gather(3, 0)
        gather(2, 1)
        expo(3, 0)
        negate(3, 1)
        turn_col(2, 0)
        recip(3, 0)
        weigh(2, 1)
        negate(3, 3)
        recip(3, 2)
        uv(1)
        weigh(2, 3)
        gather(0, 0)
        turn_col(2, 1)
        uv(0)
        expo(3, 1)
        turn_col(2, 2)
        turn_col(2, 3)
        gather(1, 1)
        expo(3, 3)
        weigh(3, 0)
        recip(3, 1)
        gather(0, 1)
        weigh(3, 1)
        gather(1, 2)
        colsum(2)
        recip(3, 3)
        gather(0, 2)
        weigh(3, 2)
        uv(2)
        weigh(3, 3)
        turn_col(3, 0)
        turn_col(3, 1)
        turn_col(3, 2)
        turn_col(3, 3)
        gather(3, 1)
        gather(2, 2)
        gather(3, 2)
        gather_last(0)
        colsum(3)
        gather_last(3)
        gather_last(2)
        gather_last(1)
        keep_z(3)
        uv(3)
        split()
        keep_z(0)
        turn_vt()
        keep_z(2)
        turn_rt()
        keep_z(1)
        copy_rt()
        turn_acc(2)
        copy_vt()
        turn_acc(3)
        outer(2)
        outer(3)
        turn_acc(1)
        combine(2)
        combine(3)
        sigmoid(2)
        outer(1)
        combine(1)
        turn_acc(0)
        outer(0)
        sigmoid(3)
        store(2)
        store(3)
        combine(0)
        sigmoid(1)
        sigmoid(0)
        store(1)
        store(0)
